import numpy as np
import ml_dtypes


def mxq(x, axis, fmt="e4m3"):
    dtype, down = {"e4m3": (ml_dtypes.float8_e4m3fn, 7), "e5m2": (ml_dtypes.float8_e5m2, 14)}[fmt]
    v = np.moveaxis(np.asarray(x, np.float32).astype(ml_dtypes.bfloat16).astype(np.float64), axis, -1)
    blocks = v.reshape(v.shape[:-1] + (-1, 32))
    amax = np.abs(blocks).max(-1, keepdims=True)
    byte = np.maximum(np.where(amax > 0, np.frexp(amax)[1] - 1 + 127, 0) - down, 1)
    scale = np.exp2(byte - 127.0)
    codes = (blocks / scale).astype(np.float32).astype(dtype).astype(np.float64)
    return np.moveaxis((codes * scale).reshape(v.shape), -1, axis)


WIDE = False


def mx_kscale(k):
    if not WIDE:
        return np.ones(k)
    levels = np.array([10, -10, 5, -5, 0])
    if k % 512:
        return np.exp2(np.random.permutation(np.resize(levels, k // 32))).repeat(32)
    a = np.empty((k // 512, 16))
    for p in range(k // 512):
        a[p, :8] = np.random.permutation(np.resize(levels, 8))
        for g in range(8):
            far = levels[np.abs(levels - a[p, g]) >= 10]
            a[p, g + 8] = far[np.random.randint(len(far))]
    return np.exp2(a.ravel()).repeat(32)


def f64(x):
    return np.asarray(x).astype(np.float64)


def striped(idx):
    return np.tile(idx.reshape(-1, 16).T, (8, 1)).astype(np.uint16)


def unstriped(offs):
    return offs[:16].T.reshape(-1).astype(np.int64)


E2M1 = np.array([0.0, 0.5, 1.0, 1.5, 2.0, 3.0, 4.0, 6.0, -0.0, -0.5, -1.0, -1.5, -2.0, -3.0, -4.0, -6.0])


def pack_weight(w, fmt):
    k, n = w.shape
    w = f64(np.asarray(w, np.float32).astype(ml_dtypes.bfloat16)).reshape(k // 32, 32, n)
    amax = np.abs(w).max(1)
    if fmt == "e4m3":
        byte = np.frexp(amax)[1] - 1 + 127 - 7
    else:
        mant, ex = np.frexp(amax / 6.0)
        byte = np.where(mant > 0.5, ex, ex - 1) + 127
    byte = np.clip(np.where(amax > 0, byte, 1), 1, 254)
    scaled = (w * np.exp2(127.0 - byte)[:, None, :]).reshape(k, n).astype(np.float32)
    by_word = np.ascontiguousarray(scaled.reshape(k // 512, 128, 4, n).transpose(0, 1, 3, 2))
    if fmt == "e4m3":
        words = by_word.astype(ml_dtypes.float8_e4m3fn).view(np.uint8)
    else:
        c = by_word.astype(ml_dtypes.float4_e2m1fn).view(np.uint8) & 0xF
        words = (c[..., 0::2] | (c[..., 1::2] << 4)).reshape(k // 512, 128, 2 * n)
    return np.ascontiguousarray(words), np.ascontiguousarray(byte.astype(np.uint8).reshape(k // 512, 16, n))


def unpack_weight(words, scales, fmt):
    g, _, n = scales.shape
    words = np.ascontiguousarray(words).reshape(g, 128, n, -1)
    if fmt == "e4m3":
        vals = words.view(ml_dtypes.float8_e4m3fn).astype(np.float64)
    else:
        nib = np.empty((g, 128, n, 4), np.uint8)
        nib[..., 0::2] = words & 0xF
        nib[..., 1::2] = words >> 4
        vals = E2M1[nib]
    vals = vals * np.repeat(np.exp2(scales.astype(np.float64) - 127.0), 8, axis=1)[..., None]
    return vals.transpose(0, 1, 3, 2).reshape(g * 512, n)


def gelu(v):
    return 0.5 * v * (1.0 + np.tanh(np.sqrt(2.0 / np.pi) * (v + 0.044715 * v**3)))


K, H, N, T, S = 1024, 512, 384, 4096, 1024

def setup_inputs():
    n = np.random.standard_normal
    s = mx_kscale(K)[:, None]
    u = mx_kscale(H)[:, None]
    tab_words, tab_scales = pack_weight(n((K, T)) * s, "e4m3")
    wlo_words, wlo_scales = pack_weight(0.4 * n((K, H)) / np.sqrt(K) / s * u.T, "e2m1")
    whi_words, whi_scales = pack_weight(0.4 * n((K, H)) / np.sqrt(K) / s * u.T, "e2m1")
    return {
        "tab_words": tab_words, "tab_scales": tab_scales,
        "offs": striped(np.random.permutation(T)[:S]),
        "wc": (n((K, H)) / np.sqrt(K) / s * u.T).astype(np.float32),
        "wlo_words": wlo_words, "wlo_scales": wlo_scales,
        "whi_words": whi_words, "whi_scales": whi_scales,
        "blo": ((-0.9 + 0.15 * n(H)) * u[:, 0]).astype(np.float32),
        "bhi": ((0.9 + 0.15 * n(H)) * u[:, 0]).astype(np.float32),
        "wy": (1.5 * n((H, N)) / np.sqrt(H) / u).astype(np.float32),
        "by": (0.4 * n(N)).astype(np.float32),
    }

def reference(tab_words, tab_scales, offs, wc, wlo_words, wlo_scales, whi_words, whi_scales, blo, bhi, wy, by):
    v = unpack_weight(tab_words, tab_scales, "e4m3")[:, unstriped(offs)]
    wlo = unpack_weight(wlo_words, wlo_scales, "e2m1")
    whi = unpack_weight(whi_words, whi_scales, "e2m1")
    c = mxq(f64(wc), 0, "e4m3").T @ v
    lo = (wlo.T @ v) + f64(blo)[:, None]
    hi = (whi.T @ v) + f64(bhi)[:, None]
    h = np.minimum(np.maximum(c, lo), hi)
    y = mxq(f64(wy), 0, "e4m3").T @ mxq(h, 0, "e4m3")
    return y + f64(by)[:, None]

@@ -1,0 +1,275 @@
+from contextlib import ExitStack
+
+import concourse.mybir as mybir
+from concourse.masks import make_identity
+
+K, H, N, T, S = 1024, 512, 384, 4096, 1024
+FLOPS = 2 * 3 * K * H * S + 2 * H * N * S
+
+F32 = mybir.dt.float32
+BF16 = mybir.dt.bfloat16
+I32 = mybir.dt.int32
+U32 = mybir.dt.uint32
+U16 = mybir.dt.uint16
+U8 = mybir.dt.uint8
+E4M3X4 = mybir.dt.float8_e4m3fn_x4
+E2M1X4 = mybir.dt.float4_e2m1fn_x4
+ALU = mybir.AluOpType
+ACT = mybir.ActivationFunctionType
+
+P = 128
+PASSES = K // 512
+HALF = 512
+UNIT = 128
+GROUPS = [(0, 256), (256, 512), (512, 768), (768, 896), (896, 1024)]
+
+
+def tile_list_clamped_scenario_commands_kernel(
+    tc, tab_words, tab_scales, offs, wc, wlo_words, wlo_scales, whi_words, whi_scales, blo, bhi, wy, by, out
+):
+    nc = tc.nc
+    with ExitStack() as ctx:
+        keep = ctx.enter_context(tc.tile_pool(name="keep", bufs=1))
+        psum = ctx.enter_context(tc.psum_pool(name="psum", bufs=1))
+        banks = [psum.tile([P, 512], F32, name=f"bank{b}") for b in range(8)]
+
+        offsets = keep.tile([P, S // 16], U16, name="offsets")
+        nc.sync.dma_start(offsets[:], offs)
+
+        tab_s = keep.tile([P, T // 4], I32, name="tab_s", tag="landing_b", align_bytes=64)
+        nc.vector.memset(tab_s[:], 0)
+        bias_rows = keep.tile([P, P], F32, name="bias_rows")
+        nc.vector.memset(bias_rows[:], 0.0)
+        bs_raw = keep.tile([P, 2, PASSES, H // 4], I32, name="bs_raw")
+        nc.gpsimd.memset(bs_raw[:], 0)
+
+        identity = keep.tile([P, P], F32, name="identity")
+        make_identity(nc, identity[:])
+        bw_raw = keep.tile([P, 2, PASSES, H // 2], I32, name="bw_raw", tag="landing_a", align_bytes=64)
+        for w, words in enumerate((wlo_words, whi_words)):
+            nc.sync.dma_start(bw_raw[:, w], words.rearrange("a p e -> p a e").bitcast(I32))
+        tab_w = [keep.tile([P, T], I32, name="tab_w0", align_bytes=64)]
+        nc.sync.dma_start(tab_w[0][:], tab_words[0].rearrange("p t i -> p (t i)").bitcast(I32))
+
+        tab_scale_rows = tab_scales.bitcast(I32)
+        for q in range(4):
+            nc.scalar.dma_start(tab_s[32 * q : 32 * q + 8], tab_scale_rows[:, 4 * q : 4 * q + 4])
+        for w, b in enumerate((blo, bhi)):
+            nc.scalar.dma_start(
+                bias_rows[4 * w : 4 * w + 4].rearrange("t (h i) -> t h i", i=4),
+                b.rearrange("(h t i) -> t h i", t=4, i=4),
+            )
+        for w, scales in enumerate((wlo_scales, whi_scales)):
+            rows = scales.rearrange("a q e -> q a e").bitcast(I32)
+            for q in range(4):
+                nc.gpsimd.dma_start(bs_raw[32 * q : 32 * q + 4, w], rows[4 * q : 4 * q + 4])
+
+        nc.tensor.transpose(banks[7][:, 0:P], bias_rows[:], identity[:])
+        bias = keep.tile([P, 8], F32, name="bias")
+        nc.scalar.activation(bias[:], banks[7][:, 0:8], ACT.Identity)
+
+        bw = keep.tile([P, 2 * PASSES, H // 2], I32, name="bw", align_bytes=64)
+        nc.vector.tensor_copy(
+            out=bw[:].rearrange("p g (t h x) -> p g t h x", t=4, x=2),
+            in_=bw_raw[:].rearrange("p w a (h t x) -> p (w a) t h x", t=4, x=2),
+        )
+
+        tab_w.append(keep.tile([P, T], I32, name="tab_w1", tag="landing_a", align_bytes=64))
+        nc.sync.dma_start(tab_w[1][:], tab_words[1].rearrange("p t i -> p (t i)").bitcast(I32))
+
+        v_s = [keep.tile([P, S], U8, name=f"v_s{a}", align_bytes=64) for a in range(PASSES)]
+        nc.vector.memset(v_s[1][:].bitcast(I32), 0)
+        nc.vector.tensor_copy(v_s[0][:], tab_s[:].bitcast(U8).indirect(offsets[:]))
+        for q in range(4):
+            nc.scalar.dma_start(
+                v_s[1][32 * q : 32 * q + 4].bitcast(I32), v_s[0][32 * q + 4 : 32 * q + 8].bitcast(I32)
+            )
+        late = keep.tile([P, 4 * H * PASSES + 4 * N + 8], F32, name="late", tag="landing_b", align_bytes=64)
+        wc_raw0 = late[:, 0 : 4 * H].rearrange("p (j c) -> p j c", j=4)
+        nc.sync.dma_start(wc_raw0, wc[0:512].rearrange("(p j) c -> p j c", j=4))
+        wc_raw1 = []
+        for s in range(2):
+            piece = late[:, 4 * H + 2 * H * s : 4 * H + 2 * H * (s + 1)].rearrange("p (j c) -> p j c", j=4)
+            nc.sync.dma_start(piece, wc[512:1024, 256 * s : 256 * (s + 1)].rearrange("(p j) c -> p j c", j=4))
+            wc_raw1.append(piece)
+        wy_raw = late[:, 8 * H : 8 * H + 4 * N].rearrange("p (t n) -> p t n", t=4)
+        wy_rows = wy.rearrange("(h t i) n -> t h i n", t=4, i=4)
+        for t in range(4):
+            nc.sync.dma_start(wy_raw[:, t, :], wy_rows[t])
+
+        out_bias = late[:, 8 * H + 4 * N : 8 * H + 4 * N + 3]
+        with nc.allow_non_contiguous_dma(reason="one bias value to a partition"):
+            nc.sync.dma_start(out_bias, by.rearrange("(c p) -> p c", p=P))
+
+        v_w = keep.tile([P, PASSES, S], U32, name="v_w", align_bytes=64)
+
+        def gather_words(a, half):
+            nc.vector.tensor_copy(
+                v_w[:, a, HALF * half : HALF * (half + 1)],
+                tab_w[a][:].bitcast(U32).indirect(offsets[:, 32 * half : 32 * (half + 1)]),
+            )
+
+        def bound_pass(bank, w, t, half, a):
+            cols = slice(HALF * half, HALF * (half + 1))
+            g = PASSES * w + a
+            nc.tensor.matmul_mx(
+                out=bank[:],
+                lhsT=bw[:, g, 64 * t : 64 * (t + 1)].bitcast(U8).bitcast(E2M1X4),
+                lhsT_scale=bs[:, g, 32 * t : 32 * (t + 1)].bitcast(U8),
+                rhs=v_w[:, a, cols].bitcast(E4M3X4),
+                rhs_scale=v_s[a][:, cols],
+                start=(a == 0),
+                stop=(a == PASSES - 1),
+            )
+
+        bounds = [[keep.tile([P, 4, HALF], F32, name=f"bounds{w}{half}") for half in range(2)] for w in range(2)]
+
+        def bound_out(bank, w, t, half):
+            nc.scalar.activation(
+                bounds[w][half][:, t, :], bank[:], ACT.Identity, bias=bias[:, 4 * w + t : 4 * w + t + 1]
+            )
+
+        wt = [(w, t) for w in range(2) for t in range(4)]
+        gather_words(0, 0)
+        gather_words(0, 1)
+        bs = keep.tile([P, 2 * PASSES, H // 4], I32, name="bs", align_bytes=64)
+        nc.vector.tensor_copy(
+            out=bs[:].rearrange("p g (t h) -> p g t h", t=4),
+            in_=bs_raw[:].rearrange("p w a (h t) -> p (w a) t h", t=4),
+        )
+        for b, (w, t) in enumerate(wt):
+            bound_pass(banks[b], w, t, 0, 0)
+        gather_words(1, 0)
+        gather_words(1, 1)
+        for b, (w, t) in enumerate(wt):
+            bound_pass(banks[b], w, t, 0, 1)
+            bound_out(banks[b], w, t, 0)
+
+        wc_bf = keep.tile([P, PASSES, H * 4], BF16, name="wc_bf", align_bytes=64)
+        wc_w = keep.tile([P, PASSES, H], U32, name="wc_w", align_bytes=64)
+        wc_s = keep.tile([P, PASSES, H], U8, name="wc_s", align_bytes=64)
+
+        def round_wc(a, raw, h0, h1):
+            nc.vector.tensor_copy(
+                out=wc_bf[:, a, :].rearrange("p (t h i j) -> p t h j i", t=4, i=4, j=4)[:, :, h0:h1],
+                in_=raw.rearrange("p j (h t i) -> p t h j i", t=4, i=4),
+            )
+
+        def quantise_wc(a, c0, c1):
+            nc.vector.quantize_mx(
+                out=wc_w[:, a, c0:c1].bitcast(E4M3X4), scales=wc_s[:, a, c0:c1], in_=wc_bf[:, a, 4 * c0 : 4 * c1]
+            )
+
+        round_wc(0, wc_raw0, 0, 32)
+        round_wc(1, wc_raw1[0], 0, 16)
+        quantise_wc(0, 0, H)
+        round_wc(1, wc_raw1[1], 16, 32)
+        quantise_wc(1, 0, 256)
+        quantise_wc(1, 256, 512)
+
+        def second_bounds(n):
+            w, t = wt[n]
+            for a in range(PASSES):
+                bound_pass(banks[n % 4], w, t, 1, a)
+            bound_out(banks[n % 4], w, t, 1)
+
+        for n in range(4):
+            second_bounds(n)
+
+        wy_bf = keep.tile([P, N * 4], BF16, name="wy_bf", align_bytes=64)
+        wy_w = keep.tile([P, N], U32, name="wy_w", align_bytes=64)
+        wy_s = keep.tile([P, N], U8, name="wy_s", align_bytes=64)
+        nc.scalar.copy(
+            out=wy_bf[:].rearrange("p (c i t) -> p c t i", i=4, t=4),
+            in_=wy_raw.rearrange("p t (c i) -> p c t i", i=4),
+        )
+
+        floored = [keep.tile([P, (j1 - j0) // UNIT, 4, UNIT], F32, name=f"floored{j0}") for j0, j1 in GROUPS]
+        h_bf = keep.tile([P, S * 4], BF16, name="h_bf", align_bytes=64)
+        h_w = keep.tile([P, S], U32, name="h_w", align_bytes=64)
+        h_s = keep.tile([P, S], U8, name="h_s", align_bytes=64)
+        y = [keep.tile([P, 3, j1 - j0], F32, name=f"y{j0}") for j0, j1 in GROUPS]
+        out_rows = out.rearrange("(c p) j -> p c j", p=P)
+
+        def command(u):
+            cols = slice(UNIT * u, UNIT * (u + 1))
+            bank = banks[4 + u % 2]
+            for t in range(4):
+                for a in range(PASSES):
+                    nc.tensor.matmul_mx(
+                        out=bank[:, UNIT * t : UNIT * (t + 1)],
+                        lhsT=wc_w[:, a, P * t : P * (t + 1)].bitcast(E4M3X4),
+                        lhsT_scale=wc_s[:, a, P * t : P * (t + 1)],
+                        rhs=v_w[:, a, cols].bitcast(E4M3X4),
+                        rhs_scale=v_s[a][:, cols],
+                        start=(a == 0),
+                        stop=(a == PASSES - 1),
+                    )
+            g = min(g for g, (j0, j1) in enumerate(GROUPS) if j1 > UNIT * u)
+            lo = bounds[0][u // 4][:, :, UNIT * (u % 4) : UNIT * (u % 4 + 1)]
+            nc.vector.tensor_tensor(
+                floored[g][:, u - GROUPS[g][0] // UNIT], bank[:].rearrange("p (t n) -> p t n", t=4), lo, ALU.max
+            )
+
+        def clamp(g):
+            for u in range(GROUPS[g][0] // UNIT, GROUPS[g][1] // UNIT):
+                hi = bounds[1][u // 4][:, :, UNIT * (u % 4) : UNIT * (u % 4 + 1)]
+                nc.vector.tensor_tensor(
+                    h_bf[:, 4 * UNIT * u : 4 * UNIT * (u + 1)].rearrange("p (c i t) -> p c t i", i=4, t=4),
+                    floored[g][:, u - GROUPS[g][0] // UNIT].rearrange("p t (c i) -> p c t i", i=4),
+                    hi.rearrange("p t (c i) -> p c t i", i=4),
+                    ALU.min,
+                )
+
+        def outputs(g):
+            j0, j1 = GROUPS[g]
+            width = j1 - j0
+            nc.vector.quantize_mx(
+                out=h_w[:, j0:j1].bitcast(E4M3X4), scales=h_s[:, j0:j1], in_=h_bf[:, 4 * j0 : 4 * j1]
+            )
+            accs = []
+            for c in range(3):
+                if width == UNIT:
+                    acc = banks[6 + g % 2][:, UNIT * c : UNIT * (c + 1)]
+                else:
+                    acc = banks[6 + c // 2][:, width * (c % 2) : width * (c % 2 + 1)]
+                nc.tensor.matmul_mx(
+                    out=acc,
+                    lhsT=wy_w[:, P * c : P * (c + 1)].bitcast(E4M3X4),
+                    lhsT_scale=wy_s[:, P * c : P * (c + 1)],
+                    rhs=h_w[:, j0:j1].bitcast(E4M3X4),
+                    rhs_scale=h_s[:, j0:j1],
+                    start=True,
+                    stop=True,
+                )
+                accs.append(acc)
+            for c, acc in enumerate(accs):
+                nc.scalar.activation(y[g][:, c, :], acc, ACT.Identity, bias=out_bias[:, c : c + 1])
+            nc.sync.dma_start(out_rows[:, :, j0:j1], y[g][:])
+
+        command(0)
+        command(1)
+        second_bounds(4)
+        command(2)
+        clamp(0)
+        for c0, c1 in ((0, 256), (256, 384)):
+            nc.vector.quantize_mx(
+                out=wy_w[:, c0:c1].bitcast(E4M3X4), scales=wy_s[:, c0:c1], in_=wy_bf[:, 4 * c0 : 4 * c1]
+            )
+        second_bounds(5)
+        command(3)
+        outputs(0)
+        second_bounds(6)
+        command(4)
+        clamp(1)
+        second_bounds(7)
+        command(5)
+        outputs(1)
+        command(6)
+        clamp(2)
+        command(7)
+        outputs(2)
+        clamp(3)
+        clamp(4)
+        outputs(3)
+        outputs(4)

@@ -40,7 +40,7 @@ def tile_list_clamped_scenario_commands_kernel(
         nc.vector.memset(tab_s[:], 0)
         bias_rows = keep.tile([P, P], F32, name="bias_rows")
         nc.vector.memset(bias_rows[:], 0.0)
-        bs_raw = keep.tile([P, 2, PASSES, H // 4], I32, name="bs_raw")
+        bs_raw = keep.tile([P, 2, PASSES, H // 4], I32, name="bs_raw", tag="landing_c", align_bytes=64)
         nc.gpsimd.memset(bs_raw[:], 0)
 
         identity = keep.tile([P, P], F32, name="identity")
@@ -48,8 +48,10 @@ def tile_list_clamped_scenario_commands_kernel(
         bw_raw = keep.tile([P, 2, PASSES, H // 2], I32, name="bw_raw", tag="landing_a", align_bytes=64)
         for w, words in enumerate((wlo_words, whi_words)):
             nc.sync.dma_start(bw_raw[:, w], words.rearrange("a p e -> p a e").bitcast(I32))
-        tab_w = [keep.tile([P, T], I32, name="tab_w0", align_bytes=64)]
-        nc.sync.dma_start(tab_w[0][:], tab_words[0].rearrange("p t i -> p (t i)").bitcast(I32))
+        wy_raw = keep.tile([P, 4, N], F32, name="wy_raw")
+        wy_rows = wy.rearrange("(h t i) n -> t h i n", t=4, i=4)
+        for t in range(4):
+            nc.sync.dma_start(wy_raw[:, t, :], wy_rows[t])
 
         tab_scale_rows = tab_scales.bitcast(I32)
         for q in range(4):
@@ -62,7 +64,7 @@ def tile_list_clamped_scenario_commands_kernel(
         for w, scales in enumerate((wlo_scales, whi_scales)):
             rows = scales.rearrange("a q e -> q a e").bitcast(I32)
             for q in range(4):
-                nc.gpsimd.dma_start(bs_raw[32 * q : 32 * q + 4, w], rows[4 * q : 4 * q + 4])
+                nc.scalar.dma_start(bs_raw[32 * q : 32 * q + 4, w], rows[4 * q : 4 * q + 4])
 
         nc.tensor.transpose(banks[7][:, 0:P], bias_rows[:], identity[:])
         bias = keep.tile([P, 8], F32, name="bias")
@@ -74,8 +76,8 @@ def tile_list_clamped_scenario_commands_kernel(
             in_=bw_raw[:].rearrange("p w a (h t x) -> p (w a) t h x", t=4, x=2),
         )
 
-        tab_w.append(keep.tile([P, T], I32, name="tab_w1", tag="landing_a", align_bytes=64))
-        nc.sync.dma_start(tab_w[1][:], tab_words[1].rearrange("p t i -> p (t i)").bitcast(I32))
+        tab_w = [keep.tile([P, T], I32, name="tab_w0", tag="landing_a", align_bytes=64)]
+        nc.sync.dma_start(tab_w[0][:], tab_words[0].rearrange("p t i -> p (t i)").bitcast(I32))
 
         v_s = [keep.tile([P, S], U8, name=f"v_s{a}", align_bytes=64) for a in range(PASSES)]
         nc.vector.memset(v_s[1][:].bitcast(I32), 0)
@@ -84,7 +86,14 @@ def tile_list_clamped_scenario_commands_kernel(
             nc.scalar.dma_start(
                 v_s[1][32 * q : 32 * q + 4].bitcast(I32), v_s[0][32 * q + 4 : 32 * q + 8].bitcast(I32)
             )
-        late = keep.tile([P, 4 * H * PASSES + 4 * N + 8], F32, name="late", tag="landing_b", align_bytes=64)
+        tab_w.append(keep.tile([P, T], I32, name="tab_w1", tag="landing_b", align_bytes=64))
+        nc.sync.dma_start(tab_w[1][:], tab_words[1].rearrange("p t i -> p (t i)").bitcast(I32))
+        bs = keep.tile([P, 2 * PASSES, H // 4], I32, name="bs", align_bytes=64)
+        nc.vector.tensor_copy(
+            out=bs[:].rearrange("p g (t h) -> p g t h", t=4),
+            in_=bs_raw[:].rearrange("p w a (h t) -> p (w a) t h", t=4),
+        )
+        late = keep.tile([P, 4 * H * PASSES + 8], F32, name="late", tag="landing_c", align_bytes=64)
         wc_raw0 = late[:, 0 : 4 * H].rearrange("p (j c) -> p j c", j=4)
         nc.sync.dma_start(wc_raw0, wc[0:512].rearrange("(p j) c -> p j c", j=4))
         wc_raw1 = []
@@ -92,15 +101,22 @@ def tile_list_clamped_scenario_commands_kernel(
             piece = late[:, 4 * H + 2 * H * s : 4 * H + 2 * H * (s + 1)].rearrange("p (j c) -> p j c", j=4)
             nc.sync.dma_start(piece, wc[512:1024, 256 * s : 256 * (s + 1)].rearrange("(p j) c -> p j c", j=4))
             wc_raw1.append(piece)
-        wy_raw = late[:, 8 * H : 8 * H + 4 * N].rearrange("p (t n) -> p t n", t=4)
-        wy_rows = wy.rearrange("(h t i) n -> t h i n", t=4, i=4)
-        for t in range(4):
-            nc.sync.dma_start(wy_raw[:, t, :], wy_rows[t])
-
-        out_bias = late[:, 8 * H + 4 * N : 8 * H + 4 * N + 3]
+        out_bias = late[:, 8 * H : 8 * H + 3]
         with nc.allow_non_contiguous_dma(reason="one bias value to a partition"):
             nc.sync.dma_start(out_bias, by.rearrange("(c p) -> p c", p=P))
 
+        wy_bf = keep.tile([P, N * 4], BF16, name="wy_bf", align_bytes=64)
+        wy_w = keep.tile([P, N], U32, name="wy_w", align_bytes=64)
+        wy_s = keep.tile([P, N], U8, name="wy_s", align_bytes=64)
+        nc.scalar.copy(
+            out=wy_bf[:].rearrange("p (c i t) -> p c t i", i=4, t=4),
+            in_=wy_raw[:].rearrange("p t (c i) -> p c t i", i=4),
+        )
+
+        for c0, c1 in ((0, 256), (256, 384)):
+            nc.vector.quantize_mx(
+                out=wy_w[:, c0:c1].bitcast(E4M3X4), scales=wy_s[:, c0:c1], in_=wy_bf[:, 4 * c0 : 4 * c1]
+            )
         v_w = keep.tile([P, PASSES, S], U32, name="v_w", align_bytes=64)
 
         def gather_words(a, half):
@@ -132,11 +148,6 @@ def tile_list_clamped_scenario_commands_kernel(
         wt = [(w, t) for w in range(2) for t in range(4)]
         gather_words(0, 0)
         gather_words(0, 1)
-        bs = keep.tile([P, 2 * PASSES, H // 4], I32, name="bs", align_bytes=64)
-        nc.vector.tensor_copy(
-            out=bs[:].rearrange("p g (t h) -> p g t h", t=4),
-            in_=bs_raw[:].rearrange("p w a (h t) -> p (w a) t h", t=4),
-        )
         for b, (w, t) in enumerate(wt):
             bound_pass(banks[b], w, t, 0, 0)
         gather_words(1, 0)
@@ -175,14 +186,6 @@ def tile_list_clamped_scenario_commands_kernel(
 
         for n in range(4):
             second_bounds(n)
-
-        wy_bf = keep.tile([P, N * 4], BF16, name="wy_bf", align_bytes=64)
-        wy_w = keep.tile([P, N], U32, name="wy_w", align_bytes=64)
-        wy_s = keep.tile([P, N], U8, name="wy_s", align_bytes=64)
-        nc.scalar.copy(
-            out=wy_bf[:].rearrange("p (c i t) -> p c t i", i=4, t=4),
-            in_=wy_raw.rearrange("p t (c i) -> p c t i", i=4),
-        )
 
         floored = [keep.tile([P, (j1 - j0) // UNIT, 4, UNIT], F32, name=f"floored{j0}") for j0, j1 in GROUPS]
         h_bf = keep.tile([P, S * 4], BF16, name="h_bf", align_bytes=64)
@@ -230,7 +233,7 @@ def tile_list_clamped_scenario_commands_kernel(
             accs = []
             for c in range(3):
                 if width == UNIT:
-                    acc = banks[6 + g % 2][:, UNIT * c : UNIT * (c + 1)]
+                    acc = banks[c + 3 * (g % 2)][:, 0:UNIT]
                 else:
                     acc = banks[6 + c // 2][:, width * (c % 2) : width * (c % 2 + 1)]
                 nc.tensor.matmul_mx(
@@ -244,7 +247,10 @@ def tile_list_clamped_scenario_commands_kernel(
                 )
                 accs.append(acc)
             for c, acc in enumerate(accs):
-                nc.scalar.activation(y[g][:, c, :], acc, ACT.Identity, bias=out_bias[:, c : c + 1])
+                if g == len(GROUPS) - 1 and c == 1:
+                    nc.vector.tensor_scalar(y[g][:, c, :], acc, out_bias[:, c : c + 1], None, ALU.add)
+                else:
+                    nc.scalar.activation(y[g][:, c, :], acc, ACT.Identity, bias=out_bias[:, c : c + 1])
             nc.sync.dma_start(out_rows[:, :, j0:j1], y[g][:])
 
         command(0)
@@ -252,10 +258,6 @@ def tile_list_clamped_scenario_commands_kernel(
         second_bounds(4)
         command(2)
         clamp(0)
-        for c0, c1 in ((0, 256), (256, 384)):
-            nc.vector.quantize_mx(
-                out=wy_w[:, c0:c1].bitcast(E4M3X4), scales=wy_s[:, c0:c1], in_=wy_bf[:, 4 * c0 : 4 * c1]
-            )
         second_bounds(5)
         command(3)
         outputs(0)

@@ -109,8 +109,8 @@ def tile_list_clamped_scenario_commands_kernel(
         wy_w = keep.tile([P, N], U32, name="wy_w", align_bytes=64)
         wy_s = keep.tile([P, N], U8, name="wy_s", align_bytes=64)
         nc.scalar.copy(
-            out=wy_bf[:].rearrange("p (c i t) -> p c t i", i=4, t=4),
-            in_=wy_raw[:].rearrange("p t (c i) -> p c t i", i=4),
+            out=wy_bf[:].rearrange("p (c i t) -> p c t i", i=2, t=4),
+            in_=wy_raw[:].rearrange("p t (c i) -> p c t i", i=2),
         )
 
         for c0, c1 in ((0, 256), (256, 384)):
@@ -162,8 +162,8 @@ def tile_list_clamped_scenario_commands_kernel(
 
         def round_wc(a, raw, h0, h1):
             nc.vector.tensor_copy(
-                out=wc_bf[:, a, :].rearrange("p (t h i j) -> p t h j i", t=4, i=4, j=4)[:, :, h0:h1],
-                in_=raw.rearrange("p j (h t i) -> p t h j i", t=4, i=4),
+                out=wc_bf[:, a, :].rearrange("p (t h i j) -> p t h i j", t=4, i=4, j=4)[:, :, h0:h1],
+                in_=raw.rearrange("p j (h t i) -> p t h i j", t=4, i=4),
             )
 
         def quantise_wc(a, c0, c1):
@@ -218,9 +218,9 @@ def tile_list_clamped_scenario_commands_kernel(
             for u in range(GROUPS[g][0] // UNIT, GROUPS[g][1] // UNIT):
                 hi = bounds[1][u // 4][:, :, UNIT * (u % 4) : UNIT * (u % 4 + 1)]
                 nc.vector.tensor_tensor(
-                    h_bf[:, 4 * UNIT * u : 4 * UNIT * (u + 1)].rearrange("p (c i t) -> p c t i", i=4, t=4),
-                    floored[g][:, u - GROUPS[g][0] // UNIT].rearrange("p t (c i) -> p c t i", i=4),
-                    hi.rearrange("p t (c i) -> p c t i", i=4),
+                    h_bf[:, 4 * UNIT * u : 4 * UNIT * (u + 1)].rearrange("p (c i t) -> p c t i", i=2, t=4),
+                    floored[g][:, u - GROUPS[g][0] // UNIT].rearrange("p t (c i) -> p c t i", i=2),
+                    hi.rearrange("p t (c i) -> p c t i", i=2),
                     ALU.min,
                 )
 
@@ -259,12 +259,12 @@ def tile_list_clamped_scenario_commands_kernel(
         command(2)
         clamp(0)
         second_bounds(5)
-        command(3)
-        outputs(0)
         second_bounds(6)
+        command(3)
+        second_bounds(7)
+        outputs(0)
         command(4)
         clamp(1)
-        second_bounds(7)
         command(5)
         outputs(1)
         command(6)

@@ -20,7 +20,6 @@ ACT = mybir.ActivationFunctionType
 P = 128
 PASSES = K // 512
 HALF = 512
-UNIT = 128
 GROUPS = [(0, 256), (256, 512), (512, 768), (768, 896), (896, 1024)]
 
 
@@ -36,87 +35,82 @@ def tile_list_clamped_scenario_commands_kernel(
         offsets = keep.tile([P, S // 16], U16, name="offsets")
         nc.sync.dma_start(offsets[:], offs)
 
-        tab_s = keep.tile([P, T // 4], I32, name="tab_s", tag="landing_b", align_bytes=64)
-        nc.vector.memset(tab_s[:], 0)
-        bias_rows = keep.tile([P, P], F32, name="bias_rows")
-        nc.vector.memset(bias_rows[:], 0.0)
-        bs_raw = keep.tile([P, 2, PASSES, H // 4], I32, name="bs_raw", tag="landing_c", align_bytes=64)
-        nc.gpsimd.memset(bs_raw[:], 0)
+        bs_spread = keep.tile([P, 2, PASSES, H // 4], I32, name="bs_spread")
+        for w, scales in enumerate((wlo_scales, whi_scales)):
+            nc.sync.dma_start(bs_spread[0:P:8, w], scales.rearrange("a q e -> q a e").bitcast(I32))
+        bw_raw = [
+            keep.tile([P, PASSES, H // 2], I32, name=f"bw_raw{w}", tag=f"slot_{w}", align_bytes=64) for w in range(2)
+        ]
+        for w, words in enumerate((wlo_words, whi_words)):
+            nc.sync.dma_start(bw_raw[w][:], words.rearrange("a p e -> p a e").bitcast(I32))
 
+        tab_s = keep.tile([P, T // 4], I32, name="tab_s", align_bytes=64)
+        nc.vector.memset(tab_s[:], 0)
+        bs_raw = keep.tile([P, 2, PASSES, H // 4], I32, name="bs_raw", align_bytes=64)
+        nc.vector.memset(bs_raw[:], 0)
+        v_s = [keep.tile([P, S], U8, name=f"v_s{a}", align_bytes=64) for a in range(PASSES)]
+        nc.vector.memset(v_s[1][:].bitcast(I32), 0)
+        bias_rows = keep.tile([P, P], F32, name="bias_rows")
+        nc.gpsimd.memset(bias_rows[:], 0.0)
         identity = keep.tile([P, P], F32, name="identity")
         make_identity(nc, identity[:])
-        bw_raw = keep.tile([P, 2, PASSES, H // 2], I32, name="bw_raw", tag="landing_a", align_bytes=64)
-        for w, words in enumerate((wlo_words, whi_words)):
-            nc.sync.dma_start(bw_raw[:, w], words.rearrange("a p e -> p a e").bitcast(I32))
-        wy_raw = keep.tile([P, 4, N], F32, name="wy_raw")
-        wy_rows = wy.rearrange("(h t i) n -> t h i n", t=4, i=4)
-        for t in range(4):
-            nc.sync.dma_start(wy_raw[:, t, :], wy_rows[t])
-
-        tab_scale_rows = tab_scales.bitcast(I32)
-        for q in range(4):
-            nc.scalar.dma_start(tab_s[32 * q : 32 * q + 8], tab_scale_rows[:, 4 * q : 4 * q + 4])
         for w, b in enumerate((blo, bhi)):
-            nc.scalar.dma_start(
+            nc.gpsimd.dma_start(
                 bias_rows[4 * w : 4 * w + 4].rearrange("t (h i) -> t h i", i=4),
                 b.rearrange("(h t i) -> t h i", t=4, i=4),
             )
-        for w, scales in enumerate((wlo_scales, whi_scales)):
-            rows = scales.rearrange("a q e -> q a e").bitcast(I32)
-            for q in range(4):
-                nc.scalar.dma_start(bs_raw[32 * q : 32 * q + 4, w], rows[4 * q : 4 * q + 4])
 
-        nc.tensor.transpose(banks[7][:, 0:P], bias_rows[:], identity[:])
-        bias = keep.tile([P, 8], F32, name="bias")
-        nc.scalar.activation(bias[:], banks[7][:, 0:8], ACT.Identity)
+        tab_scale_rows = tab_scales.bitcast(I32)
+        nc.scalar.dma_start(tab_s[4:P:8], tab_scale_rows[1])
+        for q in range(4):
+            nc.scalar.dma_start(tab_s[32 * q : 32 * q + 4], tab_scale_rows[0, 4 * q : 4 * q + 4])
+        tab_w = [keep.tile([P, T], I32, name="tab_w0", tag="slot_b", align_bytes=64)]
+        nc.sync.dma_start(tab_w[0][:], tab_words[0].rearrange("p t i -> p (t i)").bitcast(I32))
+        for q in range(4):
+            nc.scalar.dma_start(bs_raw[32 * q : 32 * q + 4], bs_spread[32 * q : 32 * q + 32 : 8])
 
         bw = keep.tile([P, 2 * PASSES, H // 2], I32, name="bw", align_bytes=64)
-        nc.vector.tensor_copy(
-            out=bw[:].rearrange("p g (t h x) -> p g t h x", t=4, x=2),
-            in_=bw_raw[:].rearrange("p w a (h t x) -> p (w a) t h x", t=4, x=2),
-        )
+        for w in range(2):
+            nc.vector.tensor_copy(
+                out=bw[:, PASSES * w : PASSES * (w + 1)].rearrange("p a (t h x) -> p a t h x", t=4, x=2),
+                in_=bw_raw[w][:].rearrange("p a (h t x) -> p a t h x", t=4, x=2),
+            )
+        wc_raw = keep.tile([P, PASSES, 4, H], F32, name="wc_raw", tag="slot_0", align_bytes=64)
+        for a in range(PASSES):
+            nc.sync.dma_start(wc_raw[:, a], wc[512 * a : 512 * (a + 1)].rearrange("(p j) c -> p j c", j=4))
+        tab_w.append(keep.tile([P, T], I32, name="tab_w1", tag="slot_1", align_bytes=64))
+        nc.sync.dma_start(tab_w[1][:], tab_words[1].rearrange("p t i -> p (t i)").bitcast(I32))
 
-        tab_w = [keep.tile([P, T], I32, name="tab_w0", tag="landing_a", align_bytes=64)]
-        nc.sync.dma_start(tab_w[0][:], tab_words[0].rearrange("p t i -> p (t i)").bitcast(I32))
-
-        v_s = [keep.tile([P, S], U8, name=f"v_s{a}", align_bytes=64) for a in range(PASSES)]
-        nc.vector.memset(v_s[1][:].bitcast(I32), 0)
         nc.vector.tensor_copy(v_s[0][:], tab_s[:].bitcast(U8).indirect(offsets[:]))
         for q in range(4):
-            nc.scalar.dma_start(
-                v_s[1][32 * q : 32 * q + 4].bitcast(I32), v_s[0][32 * q + 4 : 32 * q + 8].bitcast(I32)
+            nc.sync.dma_start(
+                v_s[1][32 * q : 32 * q + 4].bitcast(I32), v_s[0][32 * q + 4 : 32 * q + 32 : 8].bitcast(I32)
             )
-        tab_w.append(keep.tile([P, T], I32, name="tab_w1", tag="landing_b", align_bytes=64))
-        nc.sync.dma_start(tab_w[1][:], tab_words[1].rearrange("p t i -> p (t i)").bitcast(I32))
+
         bs = keep.tile([P, 2 * PASSES, H // 4], I32, name="bs", align_bytes=64)
         nc.vector.tensor_copy(
             out=bs[:].rearrange("p g (t h) -> p g t h", t=4),
             in_=bs_raw[:].rearrange("p w a (h t) -> p (w a) t h", t=4),
         )
-        late = keep.tile([P, 4 * H * PASSES + 8], F32, name="late", tag="landing_c", align_bytes=64)
-        wc_raw0 = late[:, 0 : 4 * H].rearrange("p (j c) -> p j c", j=4)
-        nc.sync.dma_start(wc_raw0, wc[0:512].rearrange("(p j) c -> p j c", j=4))
-        wc_raw1 = []
-        for s in range(2):
-            piece = late[:, 4 * H + 2 * H * s : 4 * H + 2 * H * (s + 1)].rearrange("p (j c) -> p j c", j=4)
-            nc.sync.dma_start(piece, wc[512:1024, 256 * s : 256 * (s + 1)].rearrange("(p j) c -> p j c", j=4))
-            wc_raw1.append(piece)
-        out_bias = late[:, 8 * H : 8 * H + 3]
-        with nc.allow_non_contiguous_dma(reason="one bias value to a partition"):
-            nc.sync.dma_start(out_bias, by.rearrange("(c p) -> p c", p=P))
 
-        wy_bf = keep.tile([P, N * 4], BF16, name="wy_bf", align_bytes=64)
-        wy_w = keep.tile([P, N], U32, name="wy_w", align_bytes=64)
-        wy_s = keep.tile([P, N], U8, name="wy_s", align_bytes=64)
-        nc.scalar.copy(
-            out=wy_bf[:].rearrange("p (c i t) -> p c t i", i=2, t=4),
-            in_=wy_raw[:].rearrange("p t (c i) -> p c t i", i=2),
-        )
+        nc.tensor.transpose(banks[7][:, 0:P], bias_rows[:], identity[:])
+        bias = keep.tile([P, 8], F32, name="bias")
+        nc.scalar.activation(bias[:], banks[7][:, 0:8], ACT.Identity)
 
-        for c0, c1 in ((0, 256), (256, 384)):
-            nc.vector.quantize_mx(
-                out=wy_w[:, c0:c1].bitcast(E4M3X4), scales=wy_s[:, c0:c1], in_=wy_bf[:, 4 * c0 : 4 * c1]
-            )
+        wc_bf = keep.tile([P, PASSES, H * 4], BF16, name="wc_bf", align_bytes=64)
+        wc_w = keep.tile([P, PASSES, H], U32, name="wc_w", align_bytes=64)
+        wc_s = keep.tile([P, PASSES, H], U8, name="wc_s", align_bytes=64)
+
+        for a in range(PASSES):
+            for t in range(4):
+                nc.scalar.copy(
+                    out=wc_bf[:, a, 4 * P * t : 4 * P * (t + 1)].rearrange("p (h i j) -> p h i j", i=4, j=4),
+                    in_=wc_raw[:, a].rearrange("p j (h t i) -> p t h i j", t=4, i=4)[:, t],
+                )
+
+        def quantise_wc(a):
+            nc.vector.quantize_mx(out=wc_w[:, a, :].bitcast(E4M3X4), scales=wc_s[:, a, :], in_=wc_bf[:, a, :])
+
         v_w = keep.tile([P, PASSES, S], U32, name="v_w", align_bytes=64)
 
         def gather_words(a, half):
@@ -145,84 +139,64 @@ def tile_list_clamped_scenario_commands_kernel(
                 bounds[w][half][:, t, :], bank[:], ACT.Identity, bias=bias[:, 4 * w + t : 4 * w + t + 1]
             )
 
-        wt = [(w, t) for w in range(2) for t in range(4)]
         gather_words(0, 0)
         gather_words(0, 1)
-        for b, (w, t) in enumerate(wt):
-            bound_pass(banks[b], w, t, 0, 0)
-        gather_words(1, 0)
-        gather_words(1, 1)
-        for b, (w, t) in enumerate(wt):
-            bound_pass(banks[b], w, t, 0, 1)
-            bound_out(banks[b], w, t, 0)
 
-        wc_bf = keep.tile([P, PASSES, H * 4], BF16, name="wc_bf", align_bytes=64)
-        wc_w = keep.tile([P, PASSES, H], U32, name="wc_w", align_bytes=64)
-        wc_s = keep.tile([P, PASSES, H], U8, name="wc_s", align_bytes=64)
+        late = keep.tile([P, 4 * N + 8], F32, name="late", tag="slot_b", align_bytes=64)
+        wy_raw = late[:, 0 : 4 * N].rearrange("p (t n) -> p t n", t=4)
+        wy_rows = wy.rearrange("(h t i) n -> t h i n", t=4, i=4)
+        for t in range(4):
+            nc.sync.dma_start(wy_raw[:, t, :], wy_rows[t])
+        out_bias = late[:, 4 * N : 4 * N + 3]
+        with nc.allow_non_contiguous_dma(reason="one bias value to a partition"):
+            nc.sync.dma_start(out_bias, by.rearrange("(c p) -> p c", p=P))
 
-        def round_wc(a, raw, h0, h1):
-            nc.vector.tensor_copy(
-                out=wc_bf[:, a, :].rearrange("p (t h i j) -> p t h i j", t=4, i=4, j=4)[:, :, h0:h1],
-                in_=raw.rearrange("p j (h t i) -> p t h i j", t=4, i=4),
-            )
+        wy_bf = keep.tile([P, N * 4], BF16, name="wy_bf", align_bytes=64)
+        wy_w = keep.tile([P, N], U32, name="wy_w", align_bytes=64)
+        wy_s = keep.tile([P, N], U8, name="wy_s", align_bytes=64)
 
-        def quantise_wc(a, c0, c1):
-            nc.vector.quantize_mx(
-                out=wc_w[:, a, c0:c1].bitcast(E4M3X4), scales=wc_s[:, a, c0:c1], in_=wc_bf[:, a, 4 * c0 : 4 * c1]
-            )
-
-        round_wc(0, wc_raw0, 0, 32)
-        round_wc(1, wc_raw1[0], 0, 16)
-        quantise_wc(0, 0, H)
-        round_wc(1, wc_raw1[1], 16, 32)
-        quantise_wc(1, 0, 256)
-        quantise_wc(1, 256, 512)
-
-        def second_bounds(n):
-            w, t = wt[n]
-            for a in range(PASSES):
-                bound_pass(banks[n % 4], w, t, 1, a)
-            bound_out(banks[n % 4], w, t, 1)
-
-        for n in range(4):
-            second_bounds(n)
-
-        floored = [keep.tile([P, (j1 - j0) // UNIT, 4, UNIT], F32, name=f"floored{j0}") for j0, j1 in GROUPS]
+        floored = [keep.tile([P, 4, HALF], F32, name=f"floored{half}") for half in range(2)]
         h_bf = keep.tile([P, S * 4], BF16, name="h_bf", align_bytes=64)
         h_w = keep.tile([P, S], U32, name="h_w", align_bytes=64)
         h_s = keep.tile([P, S], U8, name="h_s", align_bytes=64)
         y = [keep.tile([P, 3, j1 - j0], F32, name=f"y{j0}") for j0, j1 in GROUPS]
         out_rows = out.rearrange("(c p) j -> p c j", p=P)
 
-        def command(u):
-            cols = slice(UNIT * u, UNIT * (u + 1))
-            bank = banks[4 + u % 2]
-            for t in range(4):
-                for a in range(PASSES):
-                    nc.tensor.matmul_mx(
-                        out=bank[:, UNIT * t : UNIT * (t + 1)],
-                        lhsT=wc_w[:, a, P * t : P * (t + 1)].bitcast(E4M3X4),
-                        lhsT_scale=wc_s[:, a, P * t : P * (t + 1)],
-                        rhs=v_w[:, a, cols].bitcast(E4M3X4),
-                        rhs_scale=v_s[a][:, cols],
-                        start=(a == 0),
-                        stop=(a == PASSES - 1),
-                    )
-            g = min(g for g, (j0, j1) in enumerate(GROUPS) if j1 > UNIT * u)
-            lo = bounds[0][u // 4][:, :, UNIT * (u % 4) : UNIT * (u % 4 + 1)]
-            nc.vector.tensor_tensor(
-                floored[g][:, u - GROUPS[g][0] // UNIT], bank[:].rearrange("p (t n) -> p t n", t=4), lo, ALU.max
+        def command_pass(t, half, a):
+            cols = slice(HALF * half, HALF * (half + 1))
+            nc.tensor.matmul_mx(
+                out=banks[4 + t % 2][:],
+                lhsT=wc_w[:, a, P * t : P * (t + 1)].bitcast(E4M3X4),
+                lhsT_scale=wc_s[:, a, P * t : P * (t + 1)],
+                rhs=v_w[:, a, cols].bitcast(E4M3X4),
+                rhs_scale=v_s[a][:, cols],
+                start=(a == 0),
+                stop=(a == PASSES - 1),
             )
 
+        def floor(t, half):
+            nc.vector.tensor_tensor(floored[half][:, t, :], banks[4 + t % 2][:], bounds[0][half][:, t, :], ALU.max)
+
+        def command(t, half):
+            for a in range(PASSES):
+                command_pass(t, half, a)
+            floor(t, half)
+
+        def bound(b, w, t, half):
+            for a in range(PASSES):
+                bound_pass(banks[b], w, t, half, a)
+            bound_out(banks[b], w, t, half)
+
         def clamp(g):
-            for u in range(GROUPS[g][0] // UNIT, GROUPS[g][1] // UNIT):
-                hi = bounds[1][u // 4][:, :, UNIT * (u % 4) : UNIT * (u % 4 + 1)]
-                nc.vector.tensor_tensor(
-                    h_bf[:, 4 * UNIT * u : 4 * UNIT * (u + 1)].rearrange("p (c i t) -> p c t i", i=2, t=4),
-                    floored[g][:, u - GROUPS[g][0] // UNIT].rearrange("p t (c i) -> p c t i", i=2),
-                    hi.rearrange("p t (c i) -> p c t i", i=2),
-                    ALU.min,
-                )
+            j0, j1 = GROUPS[g]
+            half = j0 // HALF
+            cols = slice(j0 - HALF * half, j1 - HALF * half)
+            nc.vector.tensor_tensor(
+                h_bf[:, 4 * j0 : 4 * j1].rearrange("p (c i t) -> p c t i", i=2, t=4),
+                floored[half][:, :, cols].rearrange("p t (c i) -> p c t i", i=2),
+                bounds[1][half][:, :, cols].rearrange("p t (c i) -> p c t i", i=2),
+                ALU.min,
+            )
 
         def outputs(g):
             j0, j1 = GROUPS[g]
@@ -232,8 +206,8 @@ def tile_list_clamped_scenario_commands_kernel(
             )
             accs = []
             for c in range(3):
-                if width == UNIT:
-                    acc = banks[c + 3 * (g % 2)][:, 0:UNIT]
+                if width == P:
+                    acc = banks[c + 3 * (g % 2)][:, 0:P]
                 else:
                     acc = banks[6 + c // 2][:, width * (c % 2) : width * (c % 2 + 1)]
                 nc.tensor.matmul_mx(
@@ -253,25 +227,57 @@ def tile_list_clamped_scenario_commands_kernel(
                     nc.scalar.activation(y[g][:, c, :], acc, ACT.Identity, bias=out_bias[:, c : c + 1])
             nc.sync.dma_start(out_rows[:, :, j0:j1], y[g][:])
 
-        command(0)
-        command(1)
-        second_bounds(4)
-        command(2)
+        quantise_wc(0)
+        for t in range(4):
+            bound_pass(banks[t], 0, t, 0, 0)
+        for t in range(2):
+            bound_pass(banks[6 + t], 1, t, 0, 0)
+        for t in range(2):
+            command_pass(t, 0, 0)
+        quantise_wc(1)
+        gather_words(1, 0)
+        gather_words(1, 1)
+        for t in range(2):
+            bound_pass(banks[t], 0, t, 0, 1)
+            bound_out(banks[t], 0, t, 0)
+            command_pass(t, 0, 1)
+            floor(t, 0)
+        for t in range(2, 4):
+            bound_pass(banks[t], 0, t, 0, 1)
+            bound_out(banks[t], 0, t, 0)
+        for t in range(2):
+            bound_pass(banks[6 + t], 1, t, 0, 1)
+            bound_out(banks[6 + t], 1, t, 0)
+            command(2 + t, 0)
+        bound(0, 1, 2, 0)
+        for a in range(PASSES):
+            bound_pass(banks[1], 1, 3, 0, a)
+        nc.vector.tensor_copy(
+            out=wy_bf[:].rearrange("p (c i t) -> p c t i", i=2, t=4),
+            in_=wy_raw.rearrange("p t (c i) -> p c t i", i=2),
+        )
+        nc.vector.tensor_scalar(bounds[1][0][:, 3, :], banks[1][:], bias[:, 7:8], None, ALU.add)
+        for c0, c1 in ((0, 256), (256, 384)):
+            nc.vector.quantize_mx(
+                out=wy_w[:, c0:c1].bitcast(E4M3X4), scales=wy_s[:, c0:c1], in_=wy_bf[:, 4 * c0 : 4 * c1]
+            )
+        for t, b in enumerate((2, 3, 6, 7)):
+            bound(b, 0, t, 1)
         clamp(0)
-        second_bounds(5)
-        second_bounds(6)
-        command(3)
-        second_bounds(7)
-        outputs(0)
-        command(4)
         clamp(1)
-        command(5)
+        command(0, 1)
+        bound(0, 1, 0, 1)
+        bound(1, 1, 1, 1)
+        command(1, 1)
+        bound(2, 1, 2, 1)
+        bound(3, 1, 3, 1)
+        outputs(0)
+        command(2, 1)
         outputs(1)
-        command(6)
+        command(3, 1)
         clamp(2)
-        command(7)
-        outputs(2)
         clamp(3)
+        outputs(2)
         clamp(4)
         outputs(3)
         outputs(4)

@@ -20,7 +20,7 @@ ACT = mybir.ActivationFunctionType
 P = 128
 PASSES = K // 512
 HALF = 512
-GROUPS = [(0, 256), (256, 512), (512, 768), (768, 896), (896, 1024)]
+GROUPS = [(0, 512), (512, 768), (768, 896), (896, 1024)]
 
 
 def tile_list_clamped_scenario_commands_kernel(
@@ -34,250 +34,239 @@ def tile_list_clamped_scenario_commands_kernel(
 
         offsets = keep.tile([P, S // 16], U16, name="offsets")
         nc.sync.dma_start(offsets[:], offs)
-
-        bs_spread = keep.tile([P, 2, PASSES, H // 4], I32, name="bs_spread")
+        tab_s = keep.tile([P, T // 4], I32, name="tab_s", align_bytes=64)
+        nc.scalar.dma_start(tab_s[0:32], tab_scales.rearrange("a q t -> (a q) t").bitcast(I32))
+        bs_raw = keep.tile([P, 2, H // 4], I32, name="bs_raw", align_bytes=64)
         for w, scales in enumerate((wlo_scales, whi_scales)):
-            nc.sync.dma_start(bs_spread[0:P:8, w], scales.rearrange("a q e -> q a e").bitcast(I32))
-        bw_raw = [
-            keep.tile([P, PASSES, H // 2], I32, name=f"bw_raw{w}", tag=f"slot_{w}", align_bytes=64) for w in range(2)
-        ]
+            nc.scalar.dma_start(bs_raw[0:32, w], scales.rearrange("a q e -> (a q) e").bitcast(I32))
+        bw_raw = [keep.tile([P, PASSES, H // 2], I32, name=f"bw_raw{w}", align_bytes=64) for w in range(2)]
         for w, words in enumerate((wlo_words, whi_words)):
             nc.sync.dma_start(bw_raw[w][:], words.rearrange("a p e -> p a e").bitcast(I32))
+        tab_w = [keep.tile([P, T], I32, name=f"tab_w{a}", tag=f"slot_tab{a}", align_bytes=64) for a in range(PASSES)]
+        for a in range(PASSES):
+            nc.sync.dma_start(tab_w[a][:], tab_words[a].rearrange("p t i -> p (t i)").bitcast(I32))
 
-        tab_s = keep.tile([P, T // 4], I32, name="tab_s", align_bytes=64)
-        nc.vector.memset(tab_s[:], 0)
-        bs_raw = keep.tile([P, 2, PASSES, H // 4], I32, name="bs_raw", align_bytes=64)
-        nc.vector.memset(bs_raw[:], 0)
-        v_s = [keep.tile([P, S], U8, name=f"v_s{a}", align_bytes=64) for a in range(PASSES)]
-        nc.vector.memset(v_s[1][:].bitcast(I32), 0)
-        bias_rows = keep.tile([P, P], F32, name="bias_rows")
-        nc.gpsimd.memset(bias_rows[:], 0.0)
+        planes = [keep.tile([P, 512], I32, name=f"planes{a}", align_bytes=64) for a in range(PASSES)]
+        for lo, hi in ((32, 64), (64, P)):
+            nc.vector.memset(tab_s[lo:hi], 0)
+        for lo, hi in ((32, 64), (64, P)):
+            nc.vector.memset(bs_raw[lo:hi], 0)
+        nc.vector.memset(planes[1][:], 0)
+
         identity = keep.tile([P, P], F32, name="identity")
         make_identity(nc, identity[:])
+        bias_rows = keep.tile([P, P], F32, name="bias_rows")
+        nc.gpsimd.memset(bias_rows[:], 0.0)
         for w, b in enumerate((blo, bhi)):
             nc.gpsimd.dma_start(
                 bias_rows[4 * w : 4 * w + 4].rearrange("t (h i) -> t h i", i=4),
                 b.rearrange("(h t i) -> t h i", t=4, i=4),
             )
+        nc.gpsimd.dma_start(bias_rows[8:11], by.rearrange("(c p) -> c p", p=P))
 
-        tab_scale_rows = tab_scales.bitcast(I32)
-        nc.scalar.dma_start(tab_s[4:P:8], tab_scale_rows[1])
+        picked_s = keep.tile([P, S], U8, name="picked_s", tag="slot_wc0", align_bytes=64)
+        nc.vector.tensor_copy(picked_s[:], tab_s[:].bitcast(U8).indirect(offsets[:]))
+        nc.vector.tensor_copy(
+            out=planes[0][:, 256:512].rearrange("p (w t h) -> p w t h", w=2, t=4),
+            in_=bs_raw[:].rearrange("p w (h t) -> p w t h", t=4),
+        )
+        nc.vector.tensor_copy(out=planes[0][:, 0:256], in_=picked_s[:].bitcast(I32))
+        for q in range(1, 4):
+            nc.scalar.dma_start(planes[0][32 * q : 32 * q + 4], planes[0][4 * q : 4 * q + 4])
         for q in range(4):
-            nc.scalar.dma_start(tab_s[32 * q : 32 * q + 4], tab_scale_rows[0, 4 * q : 4 * q + 4])
-        tab_w = [keep.tile([P, T], I32, name="tab_w0", tag="slot_b", align_bytes=64)]
-        nc.sync.dma_start(tab_w[0][:], tab_words[0].rearrange("p t i -> p (t i)").bitcast(I32))
-        for q in range(4):
-            nc.scalar.dma_start(bs_raw[32 * q : 32 * q + 4], bs_spread[32 * q : 32 * q + 32 : 8])
+            queue = nc.gpsimd if q == 3 else nc.scalar
+            queue.dma_start(planes[1][32 * q : 32 * q + 4], planes[0][16 + 4 * q : 20 + 4 * q])
 
-        bw = keep.tile([P, 2 * PASSES, H // 2], I32, name="bw", align_bytes=64)
+        wc_raw = [keep.tile([P, 4, H], F32, name="wc_raw0", tag="slot_wc0", align_bytes=64)]
+        nc.sync.dma_start(wc_raw[0][:], wc[0:512].rearrange("(p j) c -> p j c", j=4))
+
+        bw = [keep.tile([P, PASSES, H // 2], I32, name=f"bw{w}", align_bytes=64) for w in range(2)]
         for w in range(2):
             nc.vector.tensor_copy(
-                out=bw[:, PASSES * w : PASSES * (w + 1)].rearrange("p a (t h x) -> p a t h x", t=4, x=2),
+                out=bw[w][:].rearrange("p a (t h x) -> p a t h x", t=4, x=2),
                 in_=bw_raw[w][:].rearrange("p a (h t x) -> p a t h x", t=4, x=2),
             )
-        wc_raw = keep.tile([P, PASSES, 4, H], F32, name="wc_raw", tag="slot_0", align_bytes=64)
-        for a in range(PASSES):
-            nc.sync.dma_start(wc_raw[:, a], wc[512 * a : 512 * (a + 1)].rearrange("(p j) c -> p j c", j=4))
-        tab_w.append(keep.tile([P, T], I32, name="tab_w1", tag="slot_1", align_bytes=64))
-        nc.sync.dma_start(tab_w[1][:], tab_words[1].rearrange("p t i -> p (t i)").bitcast(I32))
-
-        nc.vector.tensor_copy(v_s[0][:], tab_s[:].bitcast(U8).indirect(offsets[:]))
-        for q in range(4):
-            nc.sync.dma_start(
-                v_s[1][32 * q : 32 * q + 4].bitcast(I32), v_s[0][32 * q + 4 : 32 * q + 32 : 8].bitcast(I32)
-            )
-
-        bs = keep.tile([P, 2 * PASSES, H // 4], I32, name="bs", align_bytes=64)
-        nc.vector.tensor_copy(
-            out=bs[:].rearrange("p g (t h) -> p g t h", t=4),
-            in_=bs_raw[:].rearrange("p w a (h t) -> p (w a) t h", t=4),
-        )
 
         nc.tensor.transpose(banks[7][:, 0:P], bias_rows[:], identity[:])
-        bias = keep.tile([P, 8], F32, name="bias")
-        nc.scalar.activation(bias[:], banks[7][:, 0:8], ACT.Identity)
+        bias = keep.tile([P, 16], F32, name="bias")
+        nc.scalar.activation(bias[:], banks[7][:, 0:16], ACT.Identity)
 
-        wc_bf = keep.tile([P, PASSES, H * 4], BF16, name="wc_bf", align_bytes=64)
-        wc_w = keep.tile([P, PASSES, H], U32, name="wc_w", align_bytes=64)
-        wc_s = keep.tile([P, PASSES, H], U8, name="wc_s", align_bytes=64)
-
-        for a in range(PASSES):
-            for t in range(4):
-                nc.scalar.copy(
-                    out=wc_bf[:, a, 4 * P * t : 4 * P * (t + 1)].rearrange("p (h i j) -> p h i j", i=4, j=4),
-                    in_=wc_raw[:, a].rearrange("p j (h t i) -> p t h i j", t=4, i=4)[:, t],
-                )
-
-        def quantise_wc(a):
-            nc.vector.quantize_mx(out=wc_w[:, a, :].bitcast(E4M3X4), scales=wc_s[:, a, :], in_=wc_bf[:, a, :])
-
-        v_w = keep.tile([P, PASSES, S], U32, name="v_w", align_bytes=64)
+        v_w = [[keep.tile([P, HALF], U32, name=f"v_w{a}{half}", align_bytes=64) for half in range(2)] for a in range(PASSES)]
 
         def gather_words(a, half):
             nc.vector.tensor_copy(
-                v_w[:, a, HALF * half : HALF * (half + 1)],
-                tab_w[a][:].bitcast(U32).indirect(offsets[:, 32 * half : 32 * (half + 1)]),
+                v_w[a][half][:], tab_w[a][:].bitcast(U32).indirect(offsets[:, 32 * half : 32 * (half + 1)])
             )
 
-        def bound_pass(bank, w, t, half, a):
-            cols = slice(HALF * half, HALF * (half + 1))
-            g = PASSES * w + a
+        def state_scales(a, half):
+            return planes[a][:, 128 * half : 128 * (half + 1)].bitcast(U8)
+
+        def bound_pass(b, w, t, half, a):
             nc.tensor.matmul_mx(
-                out=bank[:],
-                lhsT=bw[:, g, 64 * t : 64 * (t + 1)].bitcast(U8).bitcast(E2M1X4),
-                lhsT_scale=bs[:, g, 32 * t : 32 * (t + 1)].bitcast(U8),
-                rhs=v_w[:, a, cols].bitcast(E4M3X4),
-                rhs_scale=v_s[a][:, cols],
+                out=banks[b][:],
+                lhsT=bw[w][:, a, 64 * t : 64 * (t + 1)].bitcast(U8).bitcast(E2M1X4),
+                lhsT_scale=planes[a][:, 256 + 128 * w + 32 * t : 256 + 128 * w + 32 * (t + 1)].bitcast(U8),
+                rhs=v_w[a][half][:].bitcast(E4M3X4),
+                rhs_scale=state_scales(a, half),
                 start=(a == 0),
                 stop=(a == PASSES - 1),
             )
 
         bounds = [[keep.tile([P, 4, HALF], F32, name=f"bounds{w}{half}") for half in range(2)] for w in range(2)]
 
-        def bound_out(bank, w, t, half):
+        def bound_out(b, w, t, half):
             nc.scalar.activation(
-                bounds[w][half][:, t, :], bank[:], ACT.Identity, bias=bias[:, 4 * w + t : 4 * w + t + 1]
+                bounds[w][half][:, t, :], banks[b][:], ACT.Identity, bias=bias[:, 4 * w + t : 4 * w + t + 1]
             )
 
-        gather_words(0, 0)
-        gather_words(0, 1)
+        def bound(b, w, t, half):
+            for a in range(PASSES):
+                bound_pass(b, w, t, half, a)
+            bound_out(b, w, t, half)
 
-        late = keep.tile([P, 4 * N + 8], F32, name="late", tag="slot_b", align_bytes=64)
-        wy_raw = late[:, 0 : 4 * N].rearrange("p (t n) -> p t n", t=4)
+        for half in range(2):
+            gather_words(0, half)
+            for t in range(4):
+                bound_pass(4 * half + t, 0, t, half, 0)
+
+        wc_raw.append(keep.tile([P, 4, H], F32, name="wc_raw1", tag="slot_tab0", align_bytes=64))
+        nc.sync.dma_start(wc_raw[1][:], wc[512:1024].rearrange("(p j) c -> p j c", j=4))
+
+        for half in range(2):
+            gather_words(1, half)
+            for t in range(4):
+                bound_pass(4 * half + t, 0, t, half, 1)
+                bound_out(4 * half + t, 0, t, half)
+
+        wy_raw = keep.tile([P, 4, N], F32, name="wy_raw", tag="slot_tab1", align_bytes=64)
         wy_rows = wy.rearrange("(h t i) n -> t h i n", t=4, i=4)
         for t in range(4):
             nc.sync.dma_start(wy_raw[:, t, :], wy_rows[t])
-        out_bias = late[:, 4 * N : 4 * N + 3]
-        with nc.allow_non_contiguous_dma(reason="one bias value to a partition"):
-            nc.sync.dma_start(out_bias, by.rearrange("(c p) -> p c", p=P))
+
+        wc_bf = [keep.tile([P, H * 4], BF16, name=f"wc_bf{a}", align_bytes=64) for a in range(PASSES)]
+        wc_w = [keep.tile([P, H], U32, name=f"wc_w{a}", align_bytes=64) for a in range(PASSES)]
+        wc_s = [keep.tile([P, H], U8, name=f"wc_s{a}", align_bytes=64) for a in range(PASSES)]
+
+        def round_wc(a, t0, t1):
+            nc.vector.tensor_copy(
+                out=wc_bf[a][:].rearrange("p (t h i j) -> p t h j i", t=4, i=4, j=4)[:, t0:t1],
+                in_=wc_raw[a][:].rearrange("p j (h t i) -> p t h j i", t=4, i=4)[:, t0:t1],
+            )
+
+        def quantise_wc(a, t0, t1):
+            nc.vector.quantize_mx(
+                out=wc_w[a][:, P * t0 : P * t1].bitcast(E4M3X4),
+                scales=wc_s[a][:, P * t0 : P * t1],
+                in_=wc_bf[a][:, 4 * P * t0 : 4 * P * t1],
+            )
 
         wy_bf = keep.tile([P, N * 4], BF16, name="wy_bf", align_bytes=64)
         wy_w = keep.tile([P, N], U32, name="wy_w", align_bytes=64)
         wy_s = keep.tile([P, N], U8, name="wy_s", align_bytes=64)
 
         floored = [keep.tile([P, 4, HALF], F32, name=f"floored{half}") for half in range(2)]
-        h_bf = keep.tile([P, S * 4], BF16, name="h_bf", align_bytes=64)
-        h_w = keep.tile([P, S], U32, name="h_w", align_bytes=64)
-        h_s = keep.tile([P, S], U8, name="h_s", align_bytes=64)
+        h_bf = [keep.tile([P, (j1 - j0) * 4], BF16, name=f"h_bf{j0}", align_bytes=64) for j0, j1 in GROUPS]
+        h_w = [keep.tile([P, j1 - j0], U32, name=f"h_w{j0}", align_bytes=64) for j0, j1 in GROUPS]
+        h_s = [keep.tile([P, j1 - j0], U8, name=f"h_s{j0}", align_bytes=64) for j0, j1 in GROUPS]
         y = [keep.tile([P, 3, j1 - j0], F32, name=f"y{j0}") for j0, j1 in GROUPS]
         out_rows = out.rearrange("(c p) j -> p c j", p=P)
 
         def command_pass(t, half, a):
-            cols = slice(HALF * half, HALF * (half + 1))
             nc.tensor.matmul_mx(
-                out=banks[4 + t % 2][:],
-                lhsT=wc_w[:, a, P * t : P * (t + 1)].bitcast(E4M3X4),
-                lhsT_scale=wc_s[:, a, P * t : P * (t + 1)],
-                rhs=v_w[:, a, cols].bitcast(E4M3X4),
-                rhs_scale=v_s[a][:, cols],
+                out=banks[2 + t % 2][:],
+                lhsT=wc_w[a][:, P * t : P * (t + 1)].bitcast(E4M3X4),
+                lhsT_scale=wc_s[a][:, P * t : P * (t + 1)],
+                rhs=v_w[a][half][:].bitcast(E4M3X4),
+                rhs_scale=state_scales(a, half),
                 start=(a == 0),
                 stop=(a == PASSES - 1),
             )
 
         def floor(t, half):
-            nc.vector.tensor_tensor(floored[half][:, t, :], banks[4 + t % 2][:], bounds[0][half][:, t, :], ALU.max)
+            nc.vector.tensor_tensor(floored[half][:, t, :], banks[2 + t % 2][:], bounds[0][half][:, t, :], ALU.max)
 
         def command(t, half):
             for a in range(PASSES):
                 command_pass(t, half, a)
             floor(t, half)
 
-        def bound(b, w, t, half):
-            for a in range(PASSES):
-                bound_pass(banks[b], w, t, half, a)
-            bound_out(banks[b], w, t, half)
-
         def clamp(g):
             j0, j1 = GROUPS[g]
             half = j0 // HALF
             cols = slice(j0 - HALF * half, j1 - HALF * half)
             nc.vector.tensor_tensor(
-                h_bf[:, 4 * j0 : 4 * j1].rearrange("p (c i t) -> p c t i", i=2, t=4),
-                floored[half][:, :, cols].rearrange("p t (c i) -> p c t i", i=2),
-                bounds[1][half][:, :, cols].rearrange("p t (c i) -> p c t i", i=2),
+                h_bf[g][:].rearrange("p (c i t) -> p c t i", i=4, t=4),
+                floored[half][:, :, cols].rearrange("p t (c i) -> p c t i", i=4),
+                bounds[1][half][:, :, cols].rearrange("p t (c i) -> p c t i", i=4),
                 ALU.min,
             )
 
-        def outputs(g):
+        def quantise_h(g):
+            nc.vector.quantize_mx(out=h_w[g][:].bitcast(E4M3X4), scales=h_s[g][:], in_=h_bf[g][:])
+
+        def outputs(g, accs):
             j0, j1 = GROUPS[g]
-            width = j1 - j0
-            nc.vector.quantize_mx(
-                out=h_w[:, j0:j1].bitcast(E4M3X4), scales=h_s[:, j0:j1], in_=h_bf[:, 4 * j0 : 4 * j1]
-            )
-            accs = []
             for c in range(3):
-                if width == P:
-                    acc = banks[c + 3 * (g % 2)][:, 0:P]
-                else:
-                    acc = banks[6 + c // 2][:, width * (c % 2) : width * (c % 2 + 1)]
                 nc.tensor.matmul_mx(
-                    out=acc,
+                    out=accs[c],
                     lhsT=wy_w[:, P * c : P * (c + 1)].bitcast(E4M3X4),
                     lhsT_scale=wy_s[:, P * c : P * (c + 1)],
-                    rhs=h_w[:, j0:j1].bitcast(E4M3X4),
-                    rhs_scale=h_s[:, j0:j1],
+                    rhs=h_w[g][:].bitcast(E4M3X4),
+                    rhs_scale=h_s[g][:],
                     start=True,
                     stop=True,
                 )
-                accs.append(acc)
-            for c, acc in enumerate(accs):
+            for c in range(3):
                 if g == len(GROUPS) - 1 and c == 1:
-                    nc.vector.tensor_scalar(y[g][:, c, :], acc, out_bias[:, c : c + 1], None, ALU.add)
+                    nc.vector.tensor_scalar(y[g][:, c, :], accs[c], bias[:, 8 + c : 9 + c], None, ALU.add)
                 else:
-                    nc.scalar.activation(y[g][:, c, :], acc, ACT.Identity, bias=out_bias[:, c : c + 1])
+                    nc.scalar.activation(y[g][:, c, :], accs[c], ACT.Identity, bias=bias[:, 8 + c : 9 + c])
             nc.sync.dma_start(out_rows[:, :, j0:j1], y[g][:])
 
-        quantise_wc(0)
-        for t in range(4):
-            bound_pass(banks[t], 0, t, 0, 0)
-        for t in range(2):
-            bound_pass(banks[6 + t], 1, t, 0, 0)
+        round_wc(0, 0, 2)
+        round_wc(0, 2, 4)
+        quantise_wc(0, 0, 2)
+        quantise_wc(0, 2, 4)
+        bound(0, 1, 0, 0)
+        bound(1, 1, 1, 0)
         for t in range(2):
             command_pass(t, 0, 0)
-        quantise_wc(1)
-        gather_words(1, 0)
-        gather_words(1, 1)
+        bound(4, 1, 2, 0)
+        bound(5, 1, 3, 0)
+        round_wc(1, 0, 2)
+        round_wc(1, 2, 4)
+        quantise_wc(1, 0, 2)
+        quantise_wc(1, 2, 4)
         for t in range(2):
-            bound_pass(banks[t], 0, t, 0, 1)
-            bound_out(banks[t], 0, t, 0)
             command_pass(t, 0, 1)
             floor(t, 0)
-        for t in range(2, 4):
-            bound_pass(banks[t], 0, t, 0, 1)
-            bound_out(banks[t], 0, t, 0)
-        for t in range(2):
-            bound_pass(banks[6 + t], 1, t, 0, 1)
-            bound_out(banks[6 + t], 1, t, 0)
-            command(2 + t, 0)
-        bound(0, 1, 2, 0)
-        for a in range(PASSES):
-            bound_pass(banks[1], 1, 3, 0, a)
-        nc.vector.tensor_copy(
-            out=wy_bf[:].rearrange("p (c i t) -> p c t i", i=2, t=4),
-            in_=wy_raw.rearrange("p t (c i) -> p c t i", i=2),
+        nc.scalar.copy(
+            out=wy_bf[:].rearrange("p (c i t) -> p c t i", i=4, t=4),
+            in_=wy_raw[:].rearrange("p t (c i) -> p c t i", i=4),
         )
-        nc.vector.tensor_scalar(bounds[1][0][:, 3, :], banks[1][:], bias[:, 7:8], None, ALU.add)
+        command(2, 0)
+        bound(6, 1, 0, 1)
+        command(3, 0)
+        bound(7, 1, 1, 1)
+        clamp(0)
+        command(0, 1)
+        bound(0, 1, 2, 1)
         for c0, c1 in ((0, 256), (256, 384)):
             nc.vector.quantize_mx(
                 out=wy_w[:, c0:c1].bitcast(E4M3X4), scales=wy_s[:, c0:c1], in_=wy_bf[:, 4 * c0 : 4 * c1]
             )
-        for t, b in enumerate((2, 3, 6, 7)):
-            bound(b, 0, t, 1)
-        clamp(0)
-        clamp(1)
-        command(0, 1)
-        bound(0, 1, 0, 1)
-        bound(1, 1, 1, 1)
+        quantise_h(0)
         command(1, 1)
-        bound(2, 1, 2, 1)
-        bound(3, 1, 3, 1)
-        outputs(0)
+        bound(1, 1, 3, 1)
         command(2, 1)
-        outputs(1)
         command(3, 1)
+        outputs(0, [banks[b][:] for b in (4, 5, 6)])
+        clamp(1)
         clamp(2)
+        quantise_h(1)
+        outputs(1, [banks[7][:, 0:256], banks[7][:, 256:512], banks[0][:, 0:256]])
         clamp(3)
-        outputs(2)
-        clamp(4)
-        outputs(3)
-        outputs(4)
+        quantise_h(2)
+        outputs(2, [banks[b][:, 0:P] for b in (1, 2, 3)])
+        quantise_h(3)
+        outputs(3, [banks[b][:, 0:P] for b in (4, 5, 6)])

@@ -20,6 +20,7 @@ ACT = mybir.ActivationFunctionType
 P = 128
 PASSES = K // 512
 HALF = 512
+COMMAND_BANKS = ((0, 1, 6, 7), (2, 3, 4, 5))
 GROUPS = [(0, 512), (512, 768), (768, 896), (896, 1024)]
 
 
@@ -32,19 +33,27 @@ def tile_list_clamped_scenario_commands_kernel(
         psum = ctx.enter_context(tc.psum_pool(name="psum", bufs=1))
         banks = [psum.tile([P, 512], F32, name=f"bank{b}") for b in range(8)]
 
+        shared = ctx.enter_context(tc.tile_pool(name="shared", bufs=1))
+
         offsets = keep.tile([P, S // 16], U16, name="offsets")
         nc.sync.dma_start(offsets[:], offs)
         tab_s = keep.tile([P, T // 4], I32, name="tab_s", align_bytes=64)
-        nc.scalar.dma_start(tab_s[0:32], tab_scales.rearrange("a q t -> (a q) t").bitcast(I32))
+        nc.sync.dma_start(tab_s[0:32], tab_scales.rearrange("a q t -> (a q) t").bitcast(I32))
         bs_raw = keep.tile([P, 2, H // 4], I32, name="bs_raw", align_bytes=64)
         for w, scales in enumerate((wlo_scales, whi_scales)):
-            nc.scalar.dma_start(bs_raw[0:32, w], scales.rearrange("a q e -> (a q) e").bitcast(I32))
+            nc.sync.dma_start(bs_raw[0:32, w], scales.rearrange("a q e -> (a q) e").bitcast(I32))
         bw_raw = [keep.tile([P, PASSES, H // 2], I32, name=f"bw_raw{w}", align_bytes=64) for w in range(2)]
         for w, words in enumerate((wlo_words, whi_words)):
             nc.sync.dma_start(bw_raw[w][:], words.rearrange("a p e -> p a e").bitcast(I32))
-        tab_w = [keep.tile([P, T], I32, name=f"tab_w{a}", tag=f"slot_tab{a}", align_bytes=64) for a in range(PASSES)]
-        for a in range(PASSES):
-            nc.sync.dma_start(tab_w[a][:], tab_words[a].rearrange("p t i -> p (t i)").bitcast(I32))
+        tab_w = [shared.tile([P, T], I32, name="tab_w0", offset=0, align_bytes=64)]
+        nc.sync.dma_start(tab_w[0][:], tab_words[0].rearrange("p t i -> p (t i)").bitcast(I32))
+        bias_rows = keep.tile([P, P], F32, name="bias_rows")
+        for w, b in enumerate((blo, bhi)):
+            nc.sync.dma_start(
+                bias_rows[120 + 4 * w : 124 + 4 * w].rearrange("t (h i) -> t h i", i=4),
+                b.rearrange("(h t i) -> t h i", t=4, i=4),
+            )
+        nc.sync.dma_start(bias_rows[117:120], by.rearrange("(c p) -> c p", p=P))
 
         planes = [keep.tile([P, 512], I32, name=f"planes{a}", align_bytes=64) for a in range(PASSES)]
         for lo, hi in ((32, 64), (64, P)):
@@ -55,16 +64,9 @@ def tile_list_clamped_scenario_commands_kernel(
 
         identity = keep.tile([P, P], F32, name="identity")
         make_identity(nc, identity[:])
-        bias_rows = keep.tile([P, P], F32, name="bias_rows")
-        nc.gpsimd.memset(bias_rows[:], 0.0)
-        for w, b in enumerate((blo, bhi)):
-            nc.gpsimd.dma_start(
-                bias_rows[4 * w : 4 * w + 4].rearrange("t (h i) -> t h i", i=4),
-                b.rearrange("(h t i) -> t h i", t=4, i=4),
-            )
-        nc.gpsimd.dma_start(bias_rows[8:11], by.rearrange("(c p) -> c p", p=P))
+        nc.gpsimd.memset(bias_rows[0:117], 0.0)
 
-        picked_s = keep.tile([P, S], U8, name="picked_s", tag="slot_wc0", align_bytes=64)
+        picked_s = shared.tile([P, S], U8, name="picked_s", offset=19968, align_bytes=64)
         nc.vector.tensor_copy(picked_s[:], tab_s[:].bitcast(U8).indirect(offsets[:]))
         nc.vector.tensor_copy(
             out=planes[0][:, 256:512].rearrange("p (w t h) -> p w t h", w=2, t=4),
@@ -72,24 +74,26 @@ def tile_list_clamped_scenario_commands_kernel(
         )
         nc.vector.tensor_copy(out=planes[0][:, 0:256], in_=picked_s[:].bitcast(I32))
         for q in range(1, 4):
-            nc.scalar.dma_start(planes[0][32 * q : 32 * q + 4], planes[0][4 * q : 4 * q + 4])
+            nc.sync.dma_start(planes[0][32 * q : 32 * q + 4], planes[0][4 * q : 4 * q + 4])
+        tab_w.append(shared.tile([P, T], I32, name="tab_w1", offset=20480, align_bytes=64))
+        nc.sync.dma_start(tab_w[1][:], tab_words[1].rearrange("p t i -> p (t i)").bitcast(I32))
         for q in range(4):
-            queue = nc.gpsimd if q == 3 else nc.scalar
-            queue.dma_start(planes[1][32 * q : 32 * q + 4], planes[0][16 + 4 * q : 20 + 4 * q])
+            nc.sync.dma_start(planes[1][32 * q : 32 * q + 4], planes[0][16 + 4 * q : 20 + 4 * q])
 
-        wc_raw = [keep.tile([P, 4, H], F32, name="wc_raw0", tag="slot_wc0", align_bytes=64)]
-        nc.sync.dma_start(wc_raw[0][:], wc[0:512].rearrange("(p j) c -> p j c", j=4))
+        bw = shared.tile([P, 2, PASSES, H // 2], I32, name="bw", offset=16384, align_bytes=64)
 
-        bw = [keep.tile([P, PASSES, H // 2], I32, name=f"bw{w}", align_bytes=64) for w in range(2)]
-        for w in range(2):
+        def deal_words(w):
             nc.vector.tensor_copy(
-                out=bw[w][:].rearrange("p a (t h x) -> p a t h x", t=4, x=2),
+                out=bw[:, w].rearrange("p a (t h x) -> p a t h x", t=4, x=2),
                 in_=bw_raw[w][:].rearrange("p a (h t x) -> p a t h x", t=4, x=2),
             )
 
+        deal_words(0)
+        deal_words(1)
+
         nc.tensor.transpose(banks[7][:, 0:P], bias_rows[:], identity[:])
-        bias = keep.tile([P, 16], F32, name="bias")
-        nc.scalar.activation(bias[:], banks[7][:, 0:16], ACT.Identity)
+        bias = keep.tile([P, 12], F32, name="bias")
+        nc.scalar.activation(bias[:], banks[7][:, 116:P], ACT.Identity)
 
         v_w = [[keep.tile([P, HALF], U32, name=f"v_w{a}{half}", align_bytes=64) for half in range(2)] for a in range(PASSES)]
 
@@ -104,7 +108,7 @@ def tile_list_clamped_scenario_commands_kernel(
         def bound_pass(b, w, t, half, a):
             nc.tensor.matmul_mx(
                 out=banks[b][:],
-                lhsT=bw[w][:, a, 64 * t : 64 * (t + 1)].bitcast(U8).bitcast(E2M1X4),
+                lhsT=bw[:, w, a, 64 * t : 64 * (t + 1)].bitcast(U8).bitcast(E2M1X4),
                 lhsT_scale=planes[a][:, 256 + 128 * w + 32 * t : 256 + 128 * w + 32 * (t + 1)].bitcast(U8),
                 rhs=v_w[a][half][:].bitcast(E4M3X4),
                 rhs_scale=state_scales(a, half),
@@ -112,11 +116,11 @@ def tile_list_clamped_scenario_commands_kernel(
                 stop=(a == PASSES - 1),
             )
 
-        bounds = [[keep.tile([P, 4, HALF], F32, name=f"bounds{w}{half}") for half in range(2)] for w in range(2)]
+        bounds = [[keep.tile([P, 4, HALF], F32, name=f"bounds{w}{half}", align_bytes=64) for half in range(2)] for w in range(2)]
 
         def bound_out(b, w, t, half):
             nc.scalar.activation(
-                bounds[w][half][:, t, :], banks[b][:], ACT.Identity, bias=bias[:, 4 * w + t : 4 * w + t + 1]
+                bounds[w][half][:, t, :], banks[b][:], ACT.Identity, bias=bias[:, 4 + 4 * w + t : 5 + 4 * w + t]
             )
 
         def bound(b, w, t, half):
@@ -124,21 +128,25 @@ def tile_list_clamped_scenario_commands_kernel(
                 bound_pass(b, w, t, half, a)
             bound_out(b, w, t, half)
 
-        for half in range(2):
-            gather_words(0, half)
+        gather_words(0, 1)
+        gather_words(0, 0)
+        for w in range(2):
             for t in range(4):
-                bound_pass(4 * half + t, 0, t, half, 0)
+                bound_pass(4 * w + t, w, t, 0, 0)
 
-        wc_raw.append(keep.tile([P, 4, H], F32, name="wc_raw1", tag="slot_tab0", align_bytes=64))
-        nc.sync.dma_start(wc_raw[1][:], wc[512:1024].rearrange("(p j) c -> p j c", j=4))
+        wc_raw = [shared.tile([P, 4, H], F32, name=f"wc_raw{a}", offset=8192 * a, align_bytes=64) for a in range(PASSES)]
+        for a in range(PASSES):
+            nc.sync.dma_start(wc_raw[a][:], wc[512 * a : 512 * (a + 1)].rearrange("(p j) c -> p j c", j=4))
 
-        for half in range(2):
-            gather_words(1, half)
+        gather_words(1, 0)
+        for w in range(2):
             for t in range(4):
-                bound_pass(4 * half + t, 0, t, half, 1)
-                bound_out(4 * half + t, 0, t, half)
+                bound_pass(4 * w + t, w, t, 0, 1)
+        for t in range(4):
+            bound_out(t, 0, t, 0)
+        gather_words(1, 1)
 
-        wy_raw = keep.tile([P, 4, N], F32, name="wy_raw", tag="slot_tab1", align_bytes=64)
+        wy_raw = shared.tile([P, 4, N], F32, name="wy_raw", offset=20480, align_bytes=64)
         wy_rows = wy.rearrange("(h t i) n -> t h i n", t=4, i=4)
         for t in range(4):
             nc.sync.dma_start(wy_raw[:, t, :], wy_rows[t])
@@ -147,8 +155,8 @@ def tile_list_clamped_scenario_commands_kernel(
         wc_w = [keep.tile([P, H], U32, name=f"wc_w{a}", align_bytes=64) for a in range(PASSES)]
         wc_s = [keep.tile([P, H], U8, name=f"wc_s{a}", align_bytes=64) for a in range(PASSES)]
 
-        def round_wc(a, t0, t1):
-            nc.vector.tensor_copy(
+        def round_wc(a, t0, t1, copy=nc.vector.tensor_copy):
+            copy(
                 out=wc_bf[a][:].rearrange("p (t h i j) -> p t h j i", t=4, i=4, j=4)[:, t0:t1],
                 in_=wc_raw[a][:].rearrange("p j (h t i) -> p t h j i", t=4, i=4)[:, t0:t1],
             )
@@ -161,7 +169,6 @@ def tile_list_clamped_scenario_commands_kernel(
             )
 
         wy_bf = keep.tile([P, N * 4], BF16, name="wy_bf", align_bytes=64)
-        wy_w = keep.tile([P, N], U32, name="wy_w", align_bytes=64)
         wy_s = keep.tile([P, N], U8, name="wy_s", align_bytes=64)
 
         floored = [keep.tile([P, 4, HALF], F32, name=f"floored{half}") for half in range(2)]
@@ -171,23 +178,23 @@ def tile_list_clamped_scenario_commands_kernel(
         y = [keep.tile([P, 3, j1 - j0], F32, name=f"y{j0}") for j0, j1 in GROUPS]
         out_rows = out.rearrange("(c p) j -> p c j", p=P)
 
-        def command_pass(t, half, a):
+        def command_pass(t, half, a, first):
             nc.tensor.matmul_mx(
-                out=banks[2 + t % 2][:],
+                out=banks[COMMAND_BANKS[half][t]][:],
                 lhsT=wc_w[a][:, P * t : P * (t + 1)].bitcast(E4M3X4),
                 lhsT_scale=wc_s[a][:, P * t : P * (t + 1)],
                 rhs=v_w[a][half][:].bitcast(E4M3X4),
                 rhs_scale=state_scales(a, half),
-                start=(a == 0),
-                stop=(a == PASSES - 1),
+                start=first,
+                stop=not first,
             )
 
         def floor(t, half):
-            nc.vector.tensor_tensor(floored[half][:, t, :], banks[2 + t % 2][:], bounds[0][half][:, t, :], ALU.max)
+            nc.vector.tensor_tensor(floored[half][:, t, :], banks[COMMAND_BANKS[half][t]][:], bounds[0][half][:, t, :], ALU.max)
 
         def command(t, half):
-            for a in range(PASSES):
-                command_pass(t, half, a)
+            command_pass(t, half, 1, True)
+            command_pass(t, half, 0, False)
             floor(t, half)
 
         def clamp(g):
@@ -218,55 +225,52 @@ def tile_list_clamped_scenario_commands_kernel(
                 )
             for c in range(3):
                 if g == len(GROUPS) - 1 and c == 1:
-                    nc.vector.tensor_scalar(y[g][:, c, :], accs[c], bias[:, 8 + c : 9 + c], None, ALU.add)
+                    nc.vector.tensor_scalar(y[g][:, c, :], accs[c], bias[:, 1 + c : 2 + c], None, ALU.add)
                 else:
-                    nc.scalar.activation(y[g][:, c, :], accs[c], ACT.Identity, bias=bias[:, 8 + c : 9 + c])
+                    nc.scalar.activation(y[g][:, c, :], accs[c], ACT.Identity, bias=bias[:, 1 + c : 2 + c])
             nc.sync.dma_start(out_rows[:, :, j0:j1], y[g][:])
 
         round_wc(0, 0, 2)
         round_wc(0, 2, 4)
         quantise_wc(0, 0, 2)
         quantise_wc(0, 2, 4)
-        bound(0, 1, 0, 0)
-        bound(1, 1, 1, 0)
         for t in range(2):
-            command_pass(t, 0, 0)
-        bound(4, 1, 2, 0)
-        bound(5, 1, 3, 0)
+            command_pass(t, 0, 0, True)
         round_wc(1, 0, 2)
         round_wc(1, 2, 4)
         quantise_wc(1, 0, 2)
         quantise_wc(1, 2, 4)
+        for t in range(4):
+            bound_out(4 + t, 1, t, 0)
         for t in range(2):
-            command_pass(t, 0, 1)
+            command_pass(t, 0, 1, False)
             floor(t, 0)
+        for t in range(2, 4):
+            command(t, 0)
+        for t in range(4):
+            bound(COMMAND_BANKS[1][t], 0, t, 1)
         nc.scalar.copy(
             out=wy_bf[:].rearrange("p (c i t) -> p c t i", i=4, t=4),
             in_=wy_raw[:].rearrange("p t (c i) -> p c t i", i=4),
         )
-        command(2, 0)
-        bound(6, 1, 0, 1)
-        command(3, 0)
-        bound(7, 1, 1, 1)
         clamp(0)
-        command(0, 1)
-        bound(0, 1, 2, 1)
+        wy_w = keep.tile([P, N], U32, name="wy_w", tag="bounds00", align_bytes=64)
         for c0, c1 in ((0, 256), (256, 384)):
             nc.vector.quantize_mx(
                 out=wy_w[:, c0:c1].bitcast(E4M3X4), scales=wy_s[:, c0:c1], in_=wy_bf[:, 4 * c0 : 4 * c1]
             )
         quantise_h(0)
-        command(1, 1)
-        bound(1, 1, 3, 1)
-        command(2, 1)
-        command(3, 1)
-        outputs(0, [banks[b][:] for b in (4, 5, 6)])
+        for t in range(4):
+            bound(COMMAND_BANKS[0][t], 1, t, 1)
+        for t in range(4):
+            command(t, 1)
+        outputs(0, [banks[b][:] for b in (0, 1, 6)])
         clamp(1)
         clamp(2)
         quantise_h(1)
-        outputs(1, [banks[7][:, 0:256], banks[7][:, 256:512], banks[0][:, 0:256]])
+        outputs(1, [banks[7][:, 0:256], banks[7][:, 256:512], banks[2][:, 0:256]])
         clamp(3)
         quantise_h(2)
-        outputs(2, [banks[b][:, 0:P] for b in (1, 2, 3)])
+        outputs(2, [banks[b][:, 0:P] for b in (3, 4, 5)])
         quantise_h(3)
-        outputs(3, [banks[b][:, 0:P] for b in (4, 5, 6)])
+        outputs(3, [banks[b][:, 0:P] for b in (0, 1, 6)])

@@ -20,7 +20,10 @@ ACT = mybir.ActivationFunctionType
 P = 128
 PASSES = K // 512
 HALF = 512
-COMMAND_BANKS = ((0, 1, 6, 7), (2, 3, 4, 5))
+COMMAND_BANKS = ((0, 1, 4, 5), (2, 3, 6, 7))
+SECOND_LOWER_BANKS = (2, 3, 0, 1)
+SECOND_UPPER_BANKS = (4, 5, 0, 1)
+WC_PIECES = ((0, 0, 4), (1, 0, 4))
 GROUPS = [(0, 512), (512, 768), (768, 896), (896, 1024)]
 
 
@@ -47,13 +50,9 @@ def tile_list_clamped_scenario_commands_kernel(
             nc.sync.dma_start(bw_raw[w][:], words.rearrange("a p e -> p a e").bitcast(I32))
         tab_w = [shared.tile([P, T], I32, name="tab_w0", offset=0, align_bytes=64)]
         nc.sync.dma_start(tab_w[0][:], tab_words[0].rearrange("p t i -> p (t i)").bitcast(I32))
-        bias_rows = keep.tile([P, P], F32, name="bias_rows")
+        bias_raw = keep.tile([P, H], F32, name="bias_raw")
         for w, b in enumerate((blo, bhi)):
-            nc.sync.dma_start(
-                bias_rows[120 + 4 * w : 124 + 4 * w].rearrange("t (h i) -> t h i", i=4),
-                b.rearrange("(h t i) -> t h i", t=4, i=4),
-            )
-        nc.sync.dma_start(bias_rows[117:120], by.rearrange("(c p) -> c p", p=P))
+            nc.sync.dma_start(bias_raw[96 + w : 97 + w], b.rearrange("(o r) -> o r", o=1))
 
         planes = [keep.tile([P, 512], I32, name=f"planes{a}", align_bytes=64) for a in range(PASSES)]
         for lo, hi in ((32, 64), (64, P)):
@@ -62,11 +61,10 @@ def tile_list_clamped_scenario_commands_kernel(
             nc.vector.memset(bs_raw[lo:hi], 0)
         nc.vector.memset(planes[1][:], 0)
 
-        identity = keep.tile([P, P], F32, name="identity")
-        make_identity(nc, identity[:])
-        nc.gpsimd.memset(bias_rows[0:117], 0.0)
+        bias_rows = keep.tile([P, H], F32, name="bias_rows")
+        nc.gpsimd.memset(bias_rows[:], 0.0)
 
-        picked_s = shared.tile([P, S], U8, name="picked_s", offset=19968, align_bytes=64)
+        picked_s = shared.tile([P, S], U8, name="picked_s", offset=20416, align_bytes=64)
         nc.vector.tensor_copy(picked_s[:], tab_s[:].bitcast(U8).indirect(offsets[:]))
         nc.vector.tensor_copy(
             out=planes[0][:, 256:512].rearrange("p (w t h) -> p w t h", w=2, t=4),
@@ -75,7 +73,7 @@ def tile_list_clamped_scenario_commands_kernel(
         nc.vector.tensor_copy(out=planes[0][:, 0:256], in_=picked_s[:].bitcast(I32))
         for q in range(1, 4):
             nc.sync.dma_start(planes[0][32 * q : 32 * q + 4], planes[0][4 * q : 4 * q + 4])
-        tab_w.append(shared.tile([P, T], I32, name="tab_w1", offset=20480, align_bytes=64))
+        tab_w.append(shared.tile([P, T], I32, name="tab_w1", offset=21376, align_bytes=64))
         nc.sync.dma_start(tab_w[1][:], tab_words[1].rearrange("p t i -> p (t i)").bitcast(I32))
         for q in range(4):
             nc.sync.dma_start(planes[1][32 * q : 32 * q + 4], planes[0][16 + 4 * q : 20 + 4 * q])
@@ -91,9 +89,16 @@ def tile_list_clamped_scenario_commands_kernel(
         deal_words(0)
         deal_words(1)
 
-        nc.tensor.transpose(banks[7][:, 0:P], bias_rows[:], identity[:])
-        bias = keep.tile([P, 12], F32, name="bias")
-        nc.scalar.activation(bias[:], banks[7][:, 116:P], ACT.Identity)
+        identity = shared.tile([P, P], F32, name="identity", offset=20480, align_bytes=64)
+        make_identity(nc, identity[:])
+        nc.gpsimd.tensor_copy(
+            out=bias_rows[96:98].rearrange("p (t h i) -> p t h i", t=4, i=4),
+            in_=bias_raw[96:98].rearrange("p (h t i) -> p t h i", t=4, i=4),
+        )
+        for t in range(4):
+            nc.tensor.transpose(banks[7][:, P * t : P * (t + 1)], bias_rows[:, P * t : P * (t + 1)], identity[:])
+        bias = keep.tile([P, 4, 2], F32, name="bias")
+        nc.scalar.activation(bias[:], banks[7][:].rearrange("p (t x) -> p t x", t=4)[:, :, 96:98], ACT.Identity)
 
         v_w = [[keep.tile([P, HALF], U32, name=f"v_w{a}{half}", align_bytes=64) for half in range(2)] for a in range(PASSES)]
 
@@ -120,7 +125,7 @@ def tile_list_clamped_scenario_commands_kernel(
 
         def bound_out(b, w, t, half):
             nc.scalar.activation(
-                bounds[w][half][:, t, :], banks[b][:], ACT.Identity, bias=bias[:, 4 + 4 * w + t : 5 + 4 * w + t]
+                bounds[w][half][:, t, :], banks[b][:], ACT.Identity, bias=bias[:, t, w : w + 1]
             )
 
         def bound(b, w, t, half):
@@ -134,9 +139,12 @@ def tile_list_clamped_scenario_commands_kernel(
             for t in range(4):
                 bound_pass(4 * w + t, w, t, 0, 0)
 
-        wc_raw = [shared.tile([P, 4, H], F32, name=f"wc_raw{a}", offset=8192 * a, align_bytes=64) for a in range(PASSES)]
-        for a in range(PASSES):
-            nc.sync.dma_start(wc_raw[a][:], wc[512 * a : 512 * (a + 1)].rearrange("(p j) c -> p j c", j=4))
+        wc_rows = wc.rearrange("(a p j) c -> a p j c", p=P, j=4)
+        wc_raw = []
+        for a, j0, j1 in WC_PIECES:
+            piece = shared.tile([P, j1 - j0, H], F32, name=f"wc_raw{a}_{j0}", offset=8192 * a + 2048 * j0, align_bytes=64)
+            nc.sync.dma_start(piece[:], wc_rows[a, :, j0:j1, :])
+            wc_raw.append(piece)
 
         gather_words(1, 0)
         for w in range(2):
@@ -146,7 +154,10 @@ def tile_list_clamped_scenario_commands_kernel(
             bound_out(t, 0, t, 0)
         gather_words(1, 1)
 
-        wy_raw = shared.tile([P, 4, N], F32, name="wy_raw", offset=20480, align_bytes=64)
+        out_bias = shared.tile([P, 8], F32, name="out_bias", offset=21376 + 6144, align_bytes=64)
+        with nc.allow_non_contiguous_dma(reason="one bias value to a partition"):
+            nc.sync.dma_start(out_bias[:, 0:3], by.rearrange("(c p) -> p c", p=P))
+        wy_raw = shared.tile([P, 4, N], F32, name="wy_raw", offset=21376, align_bytes=64)
         wy_rows = wy.rearrange("(h t i) n -> t h i n", t=4, i=4)
         for t in range(4):
             nc.sync.dma_start(wy_raw[:, t, :], wy_rows[t])
@@ -155,10 +166,11 @@ def tile_list_clamped_scenario_commands_kernel(
         wc_w = [keep.tile([P, H], U32, name=f"wc_w{a}", align_bytes=64) for a in range(PASSES)]
         wc_s = [keep.tile([P, H], U8, name=f"wc_s{a}", align_bytes=64) for a in range(PASSES)]
 
-        def round_wc(a, t0, t1, copy=nc.vector.tensor_copy):
-            copy(
-                out=wc_bf[a][:].rearrange("p (t h i j) -> p t h j i", t=4, i=4, j=4)[:, t0:t1],
-                in_=wc_raw[a][:].rearrange("p j (h t i) -> p t h j i", t=4, i=4)[:, t0:t1],
+        def round_wc(piece, t0, t1):
+            a, j0, j1 = WC_PIECES[piece]
+            nc.vector.tensor_copy(
+                out=wc_bf[a][:].rearrange("p (t h i j) -> p t h j i", t=4, i=4, j=4)[:, t0:t1, :, j0:j1],
+                in_=wc_raw[piece][:].rearrange("p j (h t i) -> p t h j i", t=4, i=4)[:, t0:t1],
             )
 
         def quantise_wc(a, t0, t1):
@@ -225,9 +237,9 @@ def tile_list_clamped_scenario_commands_kernel(
                 )
             for c in range(3):
                 if g == len(GROUPS) - 1 and c == 1:
-                    nc.vector.tensor_scalar(y[g][:, c, :], accs[c], bias[:, 1 + c : 2 + c], None, ALU.add)
+                    nc.vector.tensor_scalar(y[g][:, c, :], accs[c], out_bias[:, c : c + 1], None, ALU.add)
                 else:
-                    nc.scalar.activation(y[g][:, c, :], accs[c], ACT.Identity, bias=bias[:, 1 + c : 2 + c])
+                    nc.scalar.activation(y[g][:, c, :], accs[c], ACT.Identity, bias=out_bias[:, c : c + 1])
             nc.sync.dma_start(out_rows[:, :, j0:j1], y[g][:])
 
         round_wc(0, 0, 2)
@@ -248,29 +260,31 @@ def tile_list_clamped_scenario_commands_kernel(
         for t in range(2, 4):
             command(t, 0)
         for t in range(4):
-            bound(COMMAND_BANKS[1][t], 0, t, 1)
+            bound(SECOND_LOWER_BANKS[t], 0, t, 1)
         nc.scalar.copy(
             out=wy_bf[:].rearrange("p (c i t) -> p c t i", i=4, t=4),
             in_=wy_raw[:].rearrange("p t (c i) -> p c t i", i=4),
         )
         clamp(0)
+        command(0, 1)
+        quantise_h(0)
         wy_w = keep.tile([P, N], U32, name="wy_w", tag="bounds00", align_bytes=64)
         for c0, c1 in ((0, 256), (256, 384)):
             nc.vector.quantize_mx(
                 out=wy_w[:, c0:c1].bitcast(E4M3X4), scales=wy_s[:, c0:c1], in_=wy_bf[:, 4 * c0 : 4 * c1]
             )
-        quantise_h(0)
+        command(1, 1)
         for t in range(4):
-            bound(COMMAND_BANKS[0][t], 1, t, 1)
-        for t in range(4):
-            command(t, 1)
-        outputs(0, [banks[b][:] for b in (0, 1, 6)])
+            bound(SECOND_UPPER_BANKS[t], 1, t, 1)
+        command(2, 1)
+        command(3, 1)
+        outputs(0, [banks[b][:] for b in (4, 5, 2)])
         clamp(1)
         clamp(2)
         quantise_h(1)
-        outputs(1, [banks[7][:, 0:256], banks[7][:, 256:512], banks[2][:, 0:256]])
+        outputs(1, [banks[0][:, 0:256], banks[0][:, 256:512], banks[1][:, 0:256]])
         clamp(3)
         quantise_h(2)
-        outputs(2, [banks[b][:, 0:P] for b in (3, 4, 5)])
+        outputs(2, [banks[b][:, 0:P] for b in (3, 6, 7)])
         quantise_h(3)
-        outputs(3, [banks[b][:, 0:P] for b in (0, 1, 6)])
+        outputs(3, [banks[b][:, 0:P] for b in (4, 5, 2)])

@@ -24,7 +24,7 @@ COMMAND_BANKS = ((0, 1, 4, 5), (2, 3, 6, 7))
 SECOND_LOWER_BANKS = (2, 3, 0, 1)
 SECOND_UPPER_BANKS = (4, 5, 0, 1)
 WC_PIECES = ((0, 0, 4), (1, 0, 4))
-GROUPS = [(0, 512), (512, 768), (768, 896), (896, 1024)]
+GROUPS = [(0, 512), (512, 640), (640, 768), (768, 896), (896, 1024)]
 
 
 def tile_list_clamped_scenario_commands_kernel(
@@ -236,11 +236,14 @@ def tile_list_clamped_scenario_commands_kernel(
                     stop=True,
                 )
             for c in range(3):
-                if g == len(GROUPS) - 1 and c == 1:
+                if (g, c) in ((3, 1), (3, 2), (4, 1)):
                     nc.vector.tensor_scalar(y[g][:, c, :], accs[c], out_bias[:, c : c + 1], None, ALU.add)
                 else:
                     nc.scalar.activation(y[g][:, c, :], accs[c], ACT.Identity, bias=out_bias[:, c : c + 1])
-            nc.sync.dma_start(out_rows[:, :, j0:j1], y[g][:])
+                if g == 0:
+                    nc.sync.dma_start(out_rows[:, c, j0:j1], y[g][:, c, :])
+            if g > 0:
+                nc.sync.dma_start(out_rows[:, :, j0:j1], y[g][:])
 
         round_wc(0, 0, 2)
         round_wc(0, 2, 4)
@@ -282,9 +285,12 @@ def tile_list_clamped_scenario_commands_kernel(
         clamp(1)
         clamp(2)
         quantise_h(1)
-        outputs(1, [banks[0][:, 0:256], banks[0][:, 256:512], banks[1][:, 0:256]])
+        outputs(1, [banks[b][:, 0:P] for b in (0, 1, 3)])
         clamp(3)
         quantise_h(2)
-        outputs(2, [banks[b][:, 0:P] for b in (3, 6, 7)])
+        outputs(2, [banks[b][:, 0:P] for b in (6, 7, 4)])
+        clamp(4)
         quantise_h(3)
-        outputs(3, [banks[b][:, 0:P] for b in (4, 5, 2)])
+        quantise_h(4)
+        outputs(3, [banks[b][:, 0:P] for b in (5, 2, 0)])
+        outputs(4, [banks[b][:, 0:P] for b in (1, 3, 6)])

@@ -20,11 +20,33 @@ ACT = mybir.ActivationFunctionType
 P = 128
 PASSES = K // 512
 HALF = 512
+TILES = 4
+BLOCKS = N // P
+LOWER, UPPER = 0, 1
+SCALE_ROWS = 16 * PASSES
+BIAS_ROW = 96
+
+STATE_SCALES = S // 4
+WEIGHT_SCALES = H // 4
+PLANE_WIDTH = STATE_SCALES + 2 * WEIGHT_SCALES
+
+OVERLAP = 64
+AT_FIRST_PASS = 0
+AT_DEALT_WORDS = AT_FIRST_PASS + 4 * T
+AT_IDENTITY = AT_DEALT_WORDS + 2 * PASSES * 2 * H
+AT_PICKED_SCALES = AT_IDENTITY - OVERLAP
+AT_SECOND_PASS = AT_PICKED_SCALES + S - OVERLAP
+AT_OUT_BIAS = AT_SECOND_PASS + 4 * TILES * N
+
+WC_PIECES = ((0, 0, H), (1, 0, H // 2), (1, H // 2, H))
+
 COMMAND_BANKS = ((0, 1, 4, 5), (2, 3, 6, 7))
 SECOND_LOWER_BANKS = (2, 3, 0, 1)
 SECOND_UPPER_BANKS = (4, 5, 0, 1)
-WC_PIECES = ((0, 0, 4), (1, 0, 4))
-GROUPS = [(0, 512), (512, 640), (640, 768), (768, 896), (896, 1024)]
+OUTPUT_BANKS = (4, 5, 2, 0, 1, 3, 6, 7)
+
+GROUPS = ((0, HALF),) + tuple((j0, j0 + P) for j0 in range(HALF, S, P))
+VECTOR_BLOCKS = ((3, 1), (3, 2), (4, 1))
 
 
 def tile_list_clamped_scenario_commands_kernel(
@@ -34,99 +56,103 @@ def tile_list_clamped_scenario_commands_kernel(
     with ExitStack() as ctx:
         keep = ctx.enter_context(tc.tile_pool(name="keep", bufs=1))
         psum = ctx.enter_context(tc.psum_pool(name="psum", bufs=1))
-        banks = [psum.tile([P, 512], F32, name=f"bank{b}") for b in range(8)]
-
+        banks = [psum.tile([P, HALF], F32, name=f"bank{b}") for b in range(8)]
         shared = ctx.enter_context(tc.tile_pool(name="shared", bufs=1))
 
         offsets = keep.tile([P, S // 16], U16, name="offsets")
         nc.sync.dma_start(offsets[:], offs)
         tab_s = keep.tile([P, T // 4], I32, name="tab_s", align_bytes=64)
-        nc.sync.dma_start(tab_s[0:32], tab_scales.rearrange("a q t -> (a q) t").bitcast(I32))
-        bs_raw = keep.tile([P, 2, H // 4], I32, name="bs_raw", align_bytes=64)
+        nc.sync.dma_start(tab_s[0:SCALE_ROWS], tab_scales.rearrange("a q e -> (a q) e").bitcast(I32))
+        bound_s_raw = keep.tile([P, 2, WEIGHT_SCALES], I32, name="bound_s_raw", align_bytes=64)
         for w, scales in enumerate((wlo_scales, whi_scales)):
-            nc.sync.dma_start(bs_raw[0:32, w], scales.rearrange("a q e -> (a q) e").bitcast(I32))
-        bw_raw = [keep.tile([P, PASSES, H // 2], I32, name=f"bw_raw{w}", align_bytes=64) for w in range(2)]
+            nc.sync.dma_start(bound_s_raw[0:SCALE_ROWS, w], scales.rearrange("a q e -> (a q) e").bitcast(I32))
+        bound_w_raw = [keep.tile([P, PASSES, H // 2], I32, name=f"bound_w_raw{w}", align_bytes=64) for w in range(2)]
         for w, words in enumerate((wlo_words, whi_words)):
-            nc.sync.dma_start(bw_raw[w][:], words.rearrange("a p e -> p a e").bitcast(I32))
-        tab_w = [shared.tile([P, T], I32, name="tab_w0", offset=0, align_bytes=64)]
-        nc.sync.dma_start(tab_w[0][:], tab_words[0].rearrange("p t i -> p (t i)").bitcast(I32))
+            nc.sync.dma_start(bound_w_raw[w][:], words.rearrange("a p e -> p a e").bitcast(I32))
+        tab_w = [shared.tile([P, T], I32, name="tab_w0", offset=AT_FIRST_PASS, align_bytes=64)]
+        nc.sync.dma_start(tab_w[0][:], tab_words[0].rearrange("p e j -> p (e j)").bitcast(I32))
         bias_raw = keep.tile([P, H], F32, name="bias_raw")
-        for w, b in enumerate((blo, bhi)):
-            nc.sync.dma_start(bias_raw[96 + w : 97 + w], b.rearrange("(o r) -> o r", o=1))
+        for w, vector in enumerate((blo, bhi)):
+            nc.sync.dma_start(bias_raw[BIAS_ROW + w : BIAS_ROW + w + 1], vector.rearrange("(o r) -> o r", o=1))
 
-        planes = [keep.tile([P, 512], I32, name=f"planes{a}", align_bytes=64) for a in range(PASSES)]
-        for lo, hi in ((32, 64), (64, P)):
-            nc.vector.memset(tab_s[lo:hi], 0)
-        for lo, hi in ((32, 64), (64, P)):
-            nc.vector.memset(bs_raw[lo:hi], 0)
+        planes = [keep.tile([P, PLANE_WIDTH], I32, name=f"planes{a}", align_bytes=64) for a in range(PASSES)]
+        for p0, p1 in ((SCALE_ROWS, 64), (64, P)):
+            nc.vector.memset(tab_s[p0:p1], 0)
+        for p0, p1 in ((SCALE_ROWS, 64), (64, P)):
+            nc.vector.memset(bound_s_raw[p0:p1], 0)
         nc.vector.memset(planes[1][:], 0)
-
         bias_rows = keep.tile([P, H], F32, name="bias_rows")
         nc.gpsimd.memset(bias_rows[:], 0.0)
 
-        picked_s = shared.tile([P, S], U8, name="picked_s", offset=20416, align_bytes=64)
+        picked_s = shared.tile([P, S], U8, name="picked_s", offset=AT_PICKED_SCALES, align_bytes=64)
         nc.vector.tensor_copy(picked_s[:], tab_s[:].bitcast(U8).indirect(offsets[:]))
         nc.vector.tensor_copy(
-            out=planes[0][:, 256:512].rearrange("p (w t h) -> p w t h", w=2, t=4),
-            in_=bs_raw[:].rearrange("p w (h t) -> p w t h", t=4),
+            out=planes[0][:, STATE_SCALES:PLANE_WIDTH].rearrange("p (w t u) -> p w t u", w=2, t=TILES),
+            in_=bound_s_raw[:].rearrange("p w (u t) -> p w t u", t=TILES),
         )
-        nc.vector.tensor_copy(out=planes[0][:, 0:256], in_=picked_s[:].bitcast(I32))
-        for q in range(1, 4):
-            nc.sync.dma_start(planes[0][32 * q : 32 * q + 4], planes[0][4 * q : 4 * q + 4])
-        tab_w.append(shared.tile([P, T], I32, name="tab_w1", offset=21376, align_bytes=64))
-        nc.sync.dma_start(tab_w[1][:], tab_words[1].rearrange("p t i -> p (t i)").bitcast(I32))
-        for q in range(4):
-            nc.sync.dma_start(planes[1][32 * q : 32 * q + 4], planes[0][16 + 4 * q : 20 + 4 * q])
-
-        bw = shared.tile([P, 2, PASSES, H // 2], I32, name="bw", offset=16384, align_bytes=64)
-
-        def deal_words(w):
-            nc.vector.tensor_copy(
-                out=bw[:, w].rearrange("p a (t h x) -> p a t h x", t=4, x=2),
-                in_=bw_raw[w][:].rearrange("p a (h t x) -> p a t h x", t=4, x=2),
+        nc.vector.tensor_copy(out=planes[0][:, 0:STATE_SCALES], in_=picked_s[:].bitcast(I32))
+        for quadrant in range(1, 4):
+            nc.sync.dma_start(
+                planes[0][32 * quadrant : 32 * quadrant + 4], planes[0][4 * quadrant : 4 * quadrant + 4]
+            )
+        tab_w.append(shared.tile([P, T], I32, name="tab_w1", offset=AT_SECOND_PASS, align_bytes=64))
+        nc.sync.dma_start(tab_w[1][:], tab_words[1].rearrange("p e j -> p (e j)").bitcast(I32))
+        for quadrant in range(4):
+            nc.sync.dma_start(
+                planes[1][32 * quadrant : 32 * quadrant + 4], planes[0][16 + 4 * quadrant : 20 + 4 * quadrant]
             )
 
-        deal_words(0)
-        deal_words(1)
+        bound_w = shared.tile([P, 2, PASSES, H // 2], I32, name="bound_w", offset=AT_DEALT_WORDS, align_bytes=64)
+        for w in range(2):
+            nc.vector.tensor_copy(
+                out=bound_w[:, w].rearrange("p a (t u x) -> p a t u x", t=TILES, x=2),
+                in_=bound_w_raw[w][:].rearrange("p a (u t x) -> p a t u x", t=TILES, x=2),
+            )
 
-        identity = shared.tile([P, P], F32, name="identity", offset=20480, align_bytes=64)
+        identity = shared.tile([P, P], F32, name="identity", offset=AT_IDENTITY, align_bytes=64)
         make_identity(nc, identity[:])
         nc.gpsimd.tensor_copy(
-            out=bias_rows[96:98].rearrange("p (t h i) -> p t h i", t=4, i=4),
-            in_=bias_raw[96:98].rearrange("p (h t i) -> p t h i", t=4, i=4),
+            out=bias_rows[BIAS_ROW : BIAS_ROW + 2].rearrange("p (t u i) -> p t u i", t=TILES, i=4),
+            in_=bias_raw[BIAS_ROW : BIAS_ROW + 2].rearrange("p (u t i) -> p t u i", t=TILES, i=4),
         )
-        for t in range(4):
+        for t in range(TILES):
             nc.tensor.transpose(banks[7][:, P * t : P * (t + 1)], bias_rows[:, P * t : P * (t + 1)], identity[:])
-        bias = keep.tile([P, 4, 2], F32, name="bias")
-        nc.scalar.activation(bias[:], banks[7][:].rearrange("p (t x) -> p t x", t=4)[:, :, 96:98], ACT.Identity)
+        bias = keep.tile([P, TILES, 2], F32, name="bias")
+        nc.scalar.activation(
+            bias[:], banks[7][:].rearrange("p (t x) -> p t x", t=TILES)[:, :, BIAS_ROW : BIAS_ROW + 2], ACT.Identity
+        )
 
-        v_w = [[keep.tile([P, HALF], U32, name=f"v_w{a}{half}", align_bytes=64) for half in range(2)] for a in range(PASSES)]
+        v_w = [
+            [keep.tile([P, HALF], U32, name=f"v_w{a}{half}", align_bytes=64) for half in range(2)]
+            for a in range(PASSES)
+        ]
 
         def gather_words(a, half):
-            nc.vector.tensor_copy(
-                v_w[a][half][:], tab_w[a][:].bitcast(U32).indirect(offsets[:, 32 * half : 32 * (half + 1)])
-            )
+            columns = slice(HALF // 16 * half, HALF // 16 * (half + 1))
+            nc.vector.tensor_copy(v_w[a][half][:], tab_w[a][:].bitcast(U32).indirect(offsets[:, columns]))
 
         def state_scales(a, half):
-            return planes[a][:, 128 * half : 128 * (half + 1)].bitcast(U8)
+            return planes[a][:, HALF // 4 * half : HALF // 4 * (half + 1)].bitcast(U8)
 
         def bound_pass(b, w, t, half, a):
+            scales_at = STATE_SCALES + WEIGHT_SCALES * w + P // 4 * t
             nc.tensor.matmul_mx(
                 out=banks[b][:],
-                lhsT=bw[:, w, a, 64 * t : 64 * (t + 1)].bitcast(U8).bitcast(E2M1X4),
-                lhsT_scale=planes[a][:, 256 + 128 * w + 32 * t : 256 + 128 * w + 32 * (t + 1)].bitcast(U8),
+                lhsT=bound_w[:, w, a, P // 2 * t : P // 2 * (t + 1)].bitcast(U8).bitcast(E2M1X4),
+                lhsT_scale=planes[a][:, scales_at : scales_at + P // 4].bitcast(U8),
                 rhs=v_w[a][half][:].bitcast(E4M3X4),
                 rhs_scale=state_scales(a, half),
                 start=(a == 0),
                 stop=(a == PASSES - 1),
             )
 
-        bounds = [[keep.tile([P, 4, HALF], F32, name=f"bounds{w}{half}", align_bytes=64) for half in range(2)] for w in range(2)]
+        bounds = [
+            [keep.tile([P, TILES, HALF], F32, name=f"bounds{w}{half}", align_bytes=64) for half in range(2)]
+            for w in range(2)
+        ]
 
         def bound_out(b, w, t, half):
-            nc.scalar.activation(
-                bounds[w][half][:, t, :], banks[b][:], ACT.Identity, bias=bias[:, t, w : w + 1]
-            )
+            nc.scalar.activation(bounds[w][half][:, t, :], banks[b][:], ACT.Identity, bias=bias[:, t, w : w + 1])
 
         def bound(b, w, t, half):
             for a in range(PASSES):
@@ -135,31 +161,32 @@ def tile_list_clamped_scenario_commands_kernel(
 
         gather_words(0, 1)
         gather_words(0, 0)
-        for w in range(2):
-            for t in range(4):
-                bound_pass(4 * w + t, w, t, 0, 0)
+        for w in (LOWER, UPPER):
+            for t in range(TILES):
+                bound_pass(TILES * w + t, w, t, 0, 0)
 
-        wc_rows = wc.rearrange("(a p j) c -> a p j c", p=P, j=4)
+        wc_rows = wc.rearrange("(a p j) r -> a p j r", p=P, j=4)
         wc_raw = []
-        for a, j0, j1 in WC_PIECES:
-            piece = shared.tile([P, j1 - j0, H], F32, name=f"wc_raw{a}_{j0}", offset=8192 * a + 2048 * j0, align_bytes=64)
-            nc.sync.dma_start(piece[:], wc_rows[a, :, j0:j1, :])
+        for a, r0, r1 in WC_PIECES:
+            at = AT_FIRST_PASS + 4 * 4 * (H * a + r0)
+            piece = shared.tile([P, 4, r1 - r0], F32, name=f"wc_raw{a}_{r0}", offset=at, align_bytes=64)
+            nc.sync.dma_start(piece[:], wc_rows[a, :, :, r0:r1])
             wc_raw.append(piece)
 
         gather_words(1, 0)
-        for w in range(2):
-            for t in range(4):
-                bound_pass(4 * w + t, w, t, 0, 1)
-        for t in range(4):
-            bound_out(t, 0, t, 0)
+        for w in (LOWER, UPPER):
+            for t in range(TILES):
+                bound_pass(TILES * w + t, w, t, 0, 1)
+        for t in range(TILES):
+            bound_out(t, LOWER, t, 0)
         gather_words(1, 1)
 
-        out_bias = shared.tile([P, 8], F32, name="out_bias", offset=21376 + 6144, align_bytes=64)
+        out_bias = shared.tile([P, 8], F32, name="out_bias", offset=AT_OUT_BIAS, align_bytes=64)
         with nc.allow_non_contiguous_dma(reason="one bias value to a partition"):
-            nc.sync.dma_start(out_bias[:, 0:3], by.rearrange("(c p) -> p c", p=P))
-        wy_raw = shared.tile([P, 4, N], F32, name="wy_raw", offset=21376, align_bytes=64)
-        wy_rows = wy.rearrange("(h t i) n -> t h i n", t=4, i=4)
-        for t in range(4):
+            nc.sync.dma_start(out_bias[:, 0:BLOCKS], by.rearrange("(c p) -> p c", p=P))
+        wy_raw = shared.tile([P, TILES, N], F32, name="wy_raw", offset=AT_SECOND_PASS, align_bytes=64)
+        wy_rows = wy.rearrange("(u t i) n -> t u i n", t=TILES, i=4)
+        for t in range(TILES):
             nc.sync.dma_start(wy_raw[:, t, :], wy_rows[t])
 
         wc_bf = [keep.tile([P, H * 4], BF16, name=f"wc_bf{a}", align_bytes=64) for a in range(PASSES)]
@@ -167,10 +194,11 @@ def tile_list_clamped_scenario_commands_kernel(
         wc_s = [keep.tile([P, H], U8, name=f"wc_s{a}", align_bytes=64) for a in range(PASSES)]
 
         def round_wc(piece, t0, t1):
-            a, j0, j1 = WC_PIECES[piece]
+            a, r0, r1 = WC_PIECES[piece]
+            dealt = wc_bf[a][:].rearrange("p (t u i j) -> p t u j i", t=TILES, i=4, j=4)
             nc.vector.tensor_copy(
-                out=wc_bf[a][:].rearrange("p (t h i j) -> p t h j i", t=4, i=4, j=4)[:, t0:t1, :, j0:j1],
-                in_=wc_raw[piece][:].rearrange("p j (h t i) -> p t h j i", t=4, i=4)[:, t0:t1],
+                out=dealt[:, t0:t1, r0 // 16 : r1 // 16],
+                in_=wc_raw[piece][:].rearrange("p j (u t i) -> p t u j i", t=TILES, i=4)[:, t0:t1],
             )
 
         def quantise_wc(a, t0, t1):
@@ -180,29 +208,31 @@ def tile_list_clamped_scenario_commands_kernel(
                 in_=wc_bf[a][:, 4 * P * t0 : 4 * P * t1],
             )
 
-        wy_bf = keep.tile([P, N * 4], BF16, name="wy_bf", align_bytes=64)
+        wy_bf = keep.tile([P, N * TILES], BF16, name="wy_bf", align_bytes=64)
         wy_s = keep.tile([P, N], U8, name="wy_s", align_bytes=64)
 
-        floored = [keep.tile([P, 4, HALF], F32, name=f"floored{half}") for half in range(2)]
-        h_bf = [keep.tile([P, (j1 - j0) * 4], BF16, name=f"h_bf{j0}", align_bytes=64) for j0, j1 in GROUPS]
+        floored = [keep.tile([P, TILES, HALF], F32, name=f"floored{half}") for half in range(2)]
+        h_bf = [keep.tile([P, (j1 - j0) * TILES], BF16, name=f"h_bf{j0}", align_bytes=64) for j0, j1 in GROUPS]
         h_w = [keep.tile([P, j1 - j0], U32, name=f"h_w{j0}", align_bytes=64) for j0, j1 in GROUPS]
         h_s = [keep.tile([P, j1 - j0], U8, name=f"h_s{j0}", align_bytes=64) for j0, j1 in GROUPS]
-        y = [keep.tile([P, 3, j1 - j0], F32, name=f"y{j0}") for j0, j1 in GROUPS]
-        out_rows = out.rearrange("(c p) j -> p c j", p=P)
+        y = [keep.tile([P, BLOCKS, j1 - j0], F32, name=f"y{j0}") for j0, j1 in GROUPS]
+        out_rows = out.rearrange("(c p) s -> p c s", p=P)
 
-        def command_pass(t, half, a, first):
+        def command_pass(t, half, a, opens):
             nc.tensor.matmul_mx(
                 out=banks[COMMAND_BANKS[half][t]][:],
                 lhsT=wc_w[a][:, P * t : P * (t + 1)].bitcast(E4M3X4),
                 lhsT_scale=wc_s[a][:, P * t : P * (t + 1)],
                 rhs=v_w[a][half][:].bitcast(E4M3X4),
                 rhs_scale=state_scales(a, half),
-                start=first,
-                stop=not first,
+                start=opens,
+                stop=not opens,
             )
 
         def floor(t, half):
-            nc.vector.tensor_tensor(floored[half][:, t, :], banks[COMMAND_BANKS[half][t]][:], bounds[0][half][:, t, :], ALU.max)
+            nc.vector.tensor_tensor(
+                floored[half][:, t, :], banks[COMMAND_BANKS[half][t]][:], bounds[LOWER][half][:, t, :], ALU.max
+            )
 
         def command(t, half):
             command_pass(t, half, 1, True)
@@ -212,22 +242,23 @@ def tile_list_clamped_scenario_commands_kernel(
         def clamp(g):
             j0, j1 = GROUPS[g]
             half = j0 // HALF
-            cols = slice(j0 - HALF * half, j1 - HALF * half)
+            columns = slice(j0 - HALF * half, j1 - HALF * half)
             nc.vector.tensor_tensor(
-                h_bf[g][:].rearrange("p (c i t) -> p c t i", i=4, t=4),
-                floored[half][:, :, cols].rearrange("p t (c i) -> p c t i", i=4),
-                bounds[1][half][:, :, cols].rearrange("p t (c i) -> p c t i", i=4),
+                h_bf[g][:].rearrange("p (m x t) -> p m t x", x=4, t=TILES),
+                floored[half][:, :, columns].rearrange("p t (m x) -> p m t x", x=4),
+                bounds[UPPER][half][:, :, columns].rearrange("p t (m x) -> p m t x", x=4),
                 ALU.min,
             )
 
         def quantise_h(g):
             nc.vector.quantize_mx(out=h_w[g][:].bitcast(E4M3X4), scales=h_s[g][:], in_=h_bf[g][:])
 
-        def outputs(g, accs):
+        def outputs(g):
             j0, j1 = GROUPS[g]
-            for c in range(3):
+            sums = [banks[OUTPUT_BANKS[(BLOCKS * g + c) % 8]][:, 0 : j1 - j0] for c in range(BLOCKS)]
+            for c in range(BLOCKS):
                 nc.tensor.matmul_mx(
-                    out=accs[c],
+                    out=sums[c],
                     lhsT=wy_w[:, P * c : P * (c + 1)].bitcast(E4M3X4),
                     lhsT_scale=wy_s[:, P * c : P * (c + 1)],
                     rhs=h_w[g][:].bitcast(E4M3X4),
@@ -235,11 +266,11 @@ def tile_list_clamped_scenario_commands_kernel(
                     start=True,
                     stop=True,
                 )
-            for c in range(3):
-                if (g, c) in ((3, 1), (3, 2), (4, 1)):
-                    nc.vector.tensor_scalar(y[g][:, c, :], accs[c], out_bias[:, c : c + 1], None, ALU.add)
+            for c in range(BLOCKS):
+                if (g, c) in VECTOR_BLOCKS:
+                    nc.vector.tensor_scalar(y[g][:, c, :], sums[c], out_bias[:, c : c + 1], None, ALU.add)
                 else:
-                    nc.scalar.activation(y[g][:, c, :], accs[c], ACT.Identity, bias=out_bias[:, c : c + 1])
+                    nc.scalar.activation(y[g][:, c, :], sums[c], ACT.Identity, bias=out_bias[:, c : c + 1])
                 if g == 0:
                     nc.sync.dma_start(out_rows[:, c, j0:j1], y[g][:, c, :])
             if g > 0:
@@ -251,46 +282,48 @@ def tile_list_clamped_scenario_commands_kernel(
         quantise_wc(0, 2, 4)
         for t in range(2):
             command_pass(t, 0, 0, True)
-        round_wc(1, 0, 2)
-        round_wc(1, 2, 4)
+        round_wc(1, 0, 4)
+        round_wc(2, 0, 2)
+        round_wc(2, 2, 4)
         quantise_wc(1, 0, 2)
         quantise_wc(1, 2, 4)
-        for t in range(4):
-            bound_out(4 + t, 1, t, 0)
+
+        for t in range(TILES):
+            bound_out(TILES + t, UPPER, t, 0)
         for t in range(2):
             command_pass(t, 0, 1, False)
             floor(t, 0)
-        for t in range(2, 4):
+        for t in range(2, TILES):
             command(t, 0)
-        for t in range(4):
-            bound(SECOND_LOWER_BANKS[t], 0, t, 1)
+        for t in range(TILES):
+            bound(SECOND_LOWER_BANKS[t], LOWER, t, 1)
         nc.scalar.copy(
-            out=wy_bf[:].rearrange("p (c i t) -> p c t i", i=4, t=4),
-            in_=wy_raw[:].rearrange("p t (c i) -> p c t i", i=4),
+            out=wy_bf[:].rearrange("p (m x t) -> p m t x", x=4, t=TILES),
+            in_=wy_raw[:].rearrange("p t (m x) -> p m t x", x=4),
         )
         clamp(0)
         command(0, 1)
         quantise_h(0)
+
         wy_w = keep.tile([P, N], U32, name="wy_w", tag="bounds00", align_bytes=64)
-        for c0, c1 in ((0, 256), (256, 384)):
+        for n0, n1 in ((0, 256), (256, N)):
             nc.vector.quantize_mx(
-                out=wy_w[:, c0:c1].bitcast(E4M3X4), scales=wy_s[:, c0:c1], in_=wy_bf[:, 4 * c0 : 4 * c1]
+                out=wy_w[:, n0:n1].bitcast(E4M3X4), scales=wy_s[:, n0:n1], in_=wy_bf[:, TILES * n0 : TILES * n1]
             )
+
         command(1, 1)
-        for t in range(4):
-            bound(SECOND_UPPER_BANKS[t], 1, t, 1)
+        for t in range(TILES):
+            bound(SECOND_UPPER_BANKS[t], UPPER, t, 1)
         command(2, 1)
         command(3, 1)
-        outputs(0, [banks[b][:] for b in (4, 5, 2)])
+        outputs(0)
         clamp(1)
-        clamp(2)
-        quantise_h(1)
-        outputs(1, [banks[b][:, 0:P] for b in (0, 1, 3)])
-        clamp(3)
-        quantise_h(2)
-        outputs(2, [banks[b][:, 0:P] for b in (6, 7, 4)])
+        for g in (1, 2):
+            clamp(g + 1)
+            quantise_h(g)
+            outputs(g)
         clamp(4)
         quantise_h(3)
         quantise_h(4)
-        outputs(3, [banks[b][:, 0:P] for b in (5, 2, 0)])
-        outputs(4, [banks[b][:, 0:P] for b in (1, 3, 6)])
+        outputs(3)
+        outputs(4)

@@ -1,7 +1,6 @@
 from contextlib import ExitStack
 
 import concourse.mybir as mybir
-from concourse.masks import make_identity
 
 K, H, N, T, S = 1024, 512, 384, 4096, 1024
 FLOPS = 2 * 3 * K * H * S + 2 * H * N * S
@@ -24,26 +23,30 @@ TILES = 4
 BLOCKS = N // P
 LOWER, UPPER = 0, 1
 SCALE_ROWS = 16 * PASSES
-BIAS_ROW = 96
+QUAD = 32
 
 STATE_SCALES = S // 4
 WEIGHT_SCALES = H // 4
 PLANE_WIDTH = STATE_SCALES + 2 * WEIGHT_SCALES
 
 OVERLAP = 64
-AT_FIRST_PASS = 0
-AT_DEALT_WORDS = AT_FIRST_PASS + 4 * T
-AT_IDENTITY = AT_DEALT_WORDS + 2 * PASSES * 2 * H
-AT_PICKED_SCALES = AT_IDENTITY - OVERLAP
+WORDS = PASSES * 2 * H
+AT_DEALT_WORDS = 0
+AT_PICKED_SCALES = AT_DEALT_WORDS + 2 * WORDS - OVERLAP
 AT_SECOND_PASS = AT_PICKED_SCALES + S - OVERLAP
-AT_OUT_BIAS = AT_SECOND_PASS + 4 * TILES * N
+AT_SCALE_ROWS = AT_SECOND_PASS + 4 * T
+AT_WC0 = AT_SCALE_ROWS + T
+AT_WLO = AT_WC0 + 16 * H - OVERLAP
+AT_WC1A = AT_WLO + WORDS - OVERLAP
+AT_WHI = AT_WC1A + 8 * H
+AT_WC1B = AT_WHI + WORDS - OVERLAP
 
 WC_PIECES = ((0, 0, H), (1, 0, H // 2), (1, H // 2, H))
+AT_WC = (AT_WC0, AT_WC1A, AT_WC1B)
 
-COMMAND_BANKS = ((0, 1, 4, 5), (2, 3, 6, 7))
-SECOND_LOWER_BANKS = (2, 3, 0, 1)
-SECOND_UPPER_BANKS = (4, 5, 0, 1)
-OUTPUT_BANKS = (4, 5, 2, 0, 1, 3, 6, 7)
+BOUND_BANKS = (((0, 1, 2, 3), (0, 1, 4, 2)), ((4, 5, 6, 7), (3, 5, 6, 2)))
+COMMAND_BANKS = ((2, 3, 5, 6), (7, 0, 1, 4))
+OUTPUT_BANKS = (7, 3, 5, 0, 6, 1, 2, 4)
 
 GROUPS = ((0, HALF),) + tuple((j0, j0 + P) for j0 in range(HALF, S, P))
 VECTOR_BLOCKS = ((3, 1), (3, 2), (4, 1))
@@ -61,28 +64,36 @@ def tile_list_clamped_scenario_commands_kernel(
 
         offsets = keep.tile([P, S // 16], U16, name="offsets")
         nc.sync.dma_start(offsets[:], offs)
-        tab_s = keep.tile([P, T // 4], I32, name="tab_s", align_bytes=64)
+        tab_s = shared.tile([P, T // 4], I32, name="tab_s", offset=AT_SCALE_ROWS, align_bytes=64)
         nc.sync.dma_start(tab_s[0:SCALE_ROWS], tab_scales.rearrange("a q e -> (a q) e").bitcast(I32))
         bound_s_raw = keep.tile([P, 2, WEIGHT_SCALES], I32, name="bound_s_raw", align_bytes=64)
         for w, scales in enumerate((wlo_scales, whi_scales)):
             nc.sync.dma_start(bound_s_raw[0:SCALE_ROWS, w], scales.rearrange("a q e -> (a q) e").bitcast(I32))
-        bound_w_raw = [keep.tile([P, PASSES, H // 2], I32, name=f"bound_w_raw{w}", align_bytes=64) for w in range(2)]
+        bound_w_raw = [
+            shared.tile([P, PASSES, H // 2], I32, name=f"bound_w_raw{w}", offset=at, align_bytes=64)
+            for w, at in enumerate((AT_WLO, AT_WHI))
+        ]
         for w, words in enumerate((wlo_words, whi_words)):
             nc.sync.dma_start(bound_w_raw[w][:], words.rearrange("a p e -> p a e").bitcast(I32))
-        tab_w = [shared.tile([P, T], I32, name="tab_w0", offset=AT_FIRST_PASS, align_bytes=64)]
+        tab_w = [keep.tile([P, T], I32, name="tab_w0", align_bytes=64)]
         nc.sync.dma_start(tab_w[0][:], tab_words[0].rearrange("p e j -> p (e j)").bitcast(I32))
-        bias_raw = keep.tile([P, H], F32, name="bias_raw")
-        for w, vector in enumerate((blo, bhi)):
-            nc.sync.dma_start(bias_raw[BIAS_ROW + w : BIAS_ROW + w + 1], vector.rearrange("(o r) -> o r", o=1))
 
-        planes = [keep.tile([P, PLANE_WIDTH], I32, name=f"planes{a}", align_bytes=64) for a in range(PASSES)]
+        bias_raw = keep.tile([P, P], F32, name="bias_raw", align_bytes=64)
+        bias_rows = keep.tile([P, 2 * P], F32, name="bias_rows", align_bytes=64)
+        nc.gpsimd.memset(bias_raw[:], 0.0)
+        nc.gpsimd.memset(bias_rows[:, P : 2 * P], 0.0)
+        for w, vector in enumerate((blo, bhi)):
+            nc.sync.dma_start(bias_raw[w:P:QUAD, :], vector.rearrange("(q x) -> q x", q=4))
+        nc.sync.dma_start(
+            bias_rows[0:P:QUAD, P : P + QUAD * BLOCKS].rearrange("q (c x) -> q c x", c=BLOCKS),
+            by.rearrange("(c q x) -> q c x", c=BLOCKS, q=4),
+        )
+
+        planes = [keep.tile([P, PLANE_WIDTH], I32, name="planes0", align_bytes=64)]
         for p0, p1 in ((SCALE_ROWS, 64), (64, P)):
             nc.vector.memset(tab_s[p0:p1], 0)
         for p0, p1 in ((SCALE_ROWS, 64), (64, P)):
-            nc.vector.memset(bound_s_raw[p0:p1], 0)
-        nc.vector.memset(planes[1][:], 0)
-        bias_rows = keep.tile([P, H], F32, name="bias_rows")
-        nc.gpsimd.memset(bias_rows[:], 0.0)
+            nc.gpsimd.memset(bound_s_raw[p0:p1], 0)
 
         picked_s = shared.tile([P, S], U8, name="picked_s", offset=AT_PICKED_SCALES, align_bytes=64)
         nc.vector.tensor_copy(picked_s[:], tab_s[:].bitcast(U8).indirect(offsets[:]))
@@ -97,6 +108,8 @@ def tile_list_clamped_scenario_commands_kernel(
             )
         tab_w.append(shared.tile([P, T], I32, name="tab_w1", offset=AT_SECOND_PASS, align_bytes=64))
         nc.sync.dma_start(tab_w[1][:], tab_words[1].rearrange("p e j -> p (e j)").bitcast(I32))
+        planes.append(shared.tile([P, PLANE_WIDTH], I32, name="planes1", offset=AT_SCALE_ROWS, align_bytes=64))
+        nc.vector.memset(planes[1][:], 0)
         for quadrant in range(4):
             nc.sync.dma_start(
                 planes[1][32 * quadrant : 32 * quadrant + 4], planes[0][16 + 4 * quadrant : 20 + 4 * quadrant]
@@ -109,19 +122,7 @@ def tile_list_clamped_scenario_commands_kernel(
                 in_=bound_w_raw[w][:].rearrange("p a (u t x) -> p a t u x", t=TILES, x=2),
             )
 
-        identity = shared.tile([P, P], F32, name="identity", offset=AT_IDENTITY, align_bytes=64)
-        make_identity(nc, identity[:])
-        nc.gpsimd.tensor_copy(
-            out=bias_rows[BIAS_ROW : BIAS_ROW + 2].rearrange("p (t u i) -> p t u i", t=TILES, i=4),
-            in_=bias_raw[BIAS_ROW : BIAS_ROW + 2].rearrange("p (u t i) -> p t u i", t=TILES, i=4),
-        )
-        for t in range(TILES):
-            nc.tensor.transpose(banks[7][:, P * t : P * (t + 1)], bias_rows[:, P * t : P * (t + 1)], identity[:])
-        bias = keep.tile([P, TILES, 2], F32, name="bias")
-        nc.scalar.activation(
-            bias[:], banks[7][:].rearrange("p (t x) -> p t x", t=TILES)[:, :, BIAS_ROW : BIAS_ROW + 2], ACT.Identity
-        )
-
+        bias = keep.tile([P, 2 * P], F32, name="bias", align_bytes=64)
         v_w = [
             [keep.tile([P, HALF], U32, name=f"v_w{a}{half}", align_bytes=64) for half in range(2)]
             for a in range(PASSES)
@@ -134,10 +135,10 @@ def tile_list_clamped_scenario_commands_kernel(
         def state_scales(a, half):
             return planes[a][:, HALF // 4 * half : HALF // 4 * (half + 1)].bitcast(U8)
 
-        def bound_pass(b, w, t, half, a):
+        def bound_pass(w, t, half, a):
             scales_at = STATE_SCALES + WEIGHT_SCALES * w + P // 4 * t
             nc.tensor.matmul_mx(
-                out=banks[b][:],
+                out=banks[BOUND_BANKS[w][half][t]][:],
                 lhsT=bound_w[:, w, a, P // 2 * t : P // 2 * (t + 1)].bitcast(U8).bitcast(E2M1X4),
                 lhsT_scale=planes[a][:, scales_at : scales_at + P // 4].bitcast(U8),
                 rhs=v_w[a][half][:].bitcast(E4M3X4),
@@ -151,24 +152,32 @@ def tile_list_clamped_scenario_commands_kernel(
             for w in range(2)
         ]
 
-        def bound_out(b, w, t, half):
-            nc.scalar.activation(bounds[w][half][:, t, :], banks[b][:], ACT.Identity, bias=bias[:, t, w : w + 1])
+        def bound_out(w, t, half):
+            column = QUAD * t + w
+            nc.scalar.activation(
+                bounds[w][half][:, t, :], banks[BOUND_BANKS[w][half][t]][:], ACT.Identity, bias=bias[:, column : column + 1]
+            )
 
-        def bound(b, w, t, half):
+        def bound(w, t, half):
             for a in range(PASSES):
-                bound_pass(b, w, t, half, a)
-            bound_out(b, w, t, half)
+                bound_pass(w, t, half, a)
+            bound_out(w, t, half)
 
         gather_words(0, 1)
         gather_words(0, 0)
         for w in (LOWER, UPPER):
             for t in range(TILES):
-                bound_pass(TILES * w + t, w, t, 0, 0)
+                bound_pass(w, t, 0, 0)
+
+        nc.vector.tensor_copy(
+            out=bias_rows[:, 0:P].rearrange("p (t u i) -> p t u i", t=TILES, i=4),
+            in_=bias_raw[:].rearrange("p (u t i) -> p t u i", t=TILES, i=4),
+        )
+        nc.vector.transpose(bias[:], bias_rows[:])
 
         wc_rows = wc.rearrange("(a p j) r -> a p j r", p=P, j=4)
         wc_raw = []
-        for a, r0, r1 in WC_PIECES:
-            at = AT_FIRST_PASS + 4 * 4 * (H * a + r0)
+        for (a, r0, r1), at in zip(WC_PIECES, AT_WC):
             piece = shared.tile([P, 4, r1 - r0], F32, name=f"wc_raw{a}_{r0}", offset=at, align_bytes=64)
             nc.sync.dma_start(piece[:], wc_rows[a, :, :, r0:r1])
             wc_raw.append(piece)
@@ -176,14 +185,14 @@ def tile_list_clamped_scenario_commands_kernel(
         gather_words(1, 0)
         for w in (LOWER, UPPER):
             for t in range(TILES):
-                bound_pass(TILES * w + t, w, t, 0, 1)
-        for t in range(TILES):
-            bound_out(t, LOWER, t, 0)
+                bound_pass(w, t, 0, 1)
+        for w in (LOWER, UPPER):
+            for t in range(TILES):
+                bound_out(w, t, 0)
         gather_words(1, 1)
+        for t in range(2):
+            bound(LOWER, t, 1)
 
-        out_bias = shared.tile([P, 8], F32, name="out_bias", offset=AT_OUT_BIAS, align_bytes=64)
-        with nc.allow_non_contiguous_dma(reason="one bias value to a partition"):
-            nc.sync.dma_start(out_bias[:, 0:BLOCKS], by.rearrange("(c p) -> p c", p=P))
         wy_raw = shared.tile([P, TILES, N], F32, name="wy_raw", offset=AT_SECOND_PASS, align_bytes=64)
         wy_rows = wy.rearrange("(u t i) n -> t u i n", t=TILES, i=4)
         for t in range(TILES):
@@ -237,7 +246,6 @@ def tile_list_clamped_scenario_commands_kernel(
         def command(t, half):
             command_pass(t, half, 1, True)
             command_pass(t, half, 0, False)
-            floor(t, half)
 
         def clamp(g):
             j0, j1 = GROUPS[g]
@@ -268,9 +276,9 @@ def tile_list_clamped_scenario_commands_kernel(
                 )
             for c in range(BLOCKS):
                 if (g, c) in VECTOR_BLOCKS:
-                    nc.vector.tensor_scalar(y[g][:, c, :], sums[c], out_bias[:, c : c + 1], None, ALU.add)
+                    nc.vector.tensor_scalar(y[g][:, c, :], sums[c], bias[:, P + QUAD * c : P + QUAD * c + 1], None, ALU.add)
                 else:
-                    nc.scalar.activation(y[g][:, c, :], sums[c], ACT.Identity, bias=out_bias[:, c : c + 1])
+                    nc.scalar.activation(y[g][:, c, :], sums[c], ACT.Identity, bias=bias[:, P + QUAD * c : P + QUAD * c + 1])
                 if g == 0:
                     nc.sync.dma_start(out_rows[:, c, j0:j1], y[g][:, c, :])
             if g > 0:
@@ -282,27 +290,31 @@ def tile_list_clamped_scenario_commands_kernel(
         quantise_wc(0, 2, 4)
         for t in range(2):
             command_pass(t, 0, 0, True)
+        bound(LOWER, 2, 1)
         round_wc(1, 0, 4)
         round_wc(2, 0, 2)
         round_wc(2, 2, 4)
         quantise_wc(1, 0, 2)
         quantise_wc(1, 2, 4)
 
-        for t in range(TILES):
-            bound_out(TILES + t, UPPER, t, 0)
         for t in range(2):
             command_pass(t, 0, 1, False)
             floor(t, 0)
         for t in range(2, TILES):
             command(t, 0)
-        for t in range(TILES):
-            bound(SECOND_LOWER_BANKS[t], LOWER, t, 1)
+            floor(t, 0)
+        bound(LOWER, 3, 1)
         nc.scalar.copy(
             out=wy_bf[:].rearrange("p (m x t) -> p m t x", x=4, t=TILES),
             in_=wy_raw[:].rearrange("p t (m x) -> p m t x", x=4),
         )
+        bound(UPPER, 0, 1)
+        for t in range(1, TILES):
+            bound(UPPER, t, 1)
+            command(t - 1, 1)
+        command(3, 1)
         clamp(0)
-        command(0, 1)
+        floor(0, 1)
         quantise_h(0)
 
         wy_w = keep.tile([P, N], U32, name="wy_w", tag="bounds00", align_bytes=64)
@@ -311,11 +323,8 @@ def tile_list_clamped_scenario_commands_kernel(
                 out=wy_w[:, n0:n1].bitcast(E4M3X4), scales=wy_s[:, n0:n1], in_=wy_bf[:, TILES * n0 : TILES * n1]
             )
 
-        command(1, 1)
-        for t in range(TILES):
-            bound(SECOND_UPPER_BANKS[t], UPPER, t, 1)
-        command(2, 1)
-        command(3, 1)
+        for t in range(1, TILES):
+            floor(t, 1)
         outputs(0)
         clamp(1)
         for g in (1, 2):

@@ -44,9 +44,9 @@ AT_WC1B = AT_WHI + WORDS - OVERLAP
 WC_PIECES = ((0, 0, H), (1, 0, H // 2), (1, H // 2, H))
 AT_WC = (AT_WC0, AT_WC1A, AT_WC1B)
 
-BOUND_BANKS = (((0, 1, 2, 3), (0, 1, 4, 2)), ((4, 5, 6, 7), (3, 5, 6, 2)))
-COMMAND_BANKS = ((2, 3, 5, 6), (7, 0, 1, 4))
-OUTPUT_BANKS = (7, 3, 5, 0, 6, 1, 2, 4)
+BOUND_BANKS = (((0, 1, 2, 3), (0, 1, 2, 3)), ((4, 5, 6, 7), (0, 1, 4, 5)))
+COMMAND_BANKS = ((2, 3, 4, 5), (6, 7, 2, 3))
+OUTPUT_BANKS = (6, 0, 1, 4, 7, 5, 2, 3)
 
 GROUPS = ((0, HALF),) + tuple((j0, j0 + P) for j0 in range(HALF, S, P))
 VECTOR_BLOCKS = ((3, 1), (3, 2), (4, 1))
@@ -239,24 +239,30 @@ def tile_list_clamped_scenario_commands_kernel(
             )
 
         def floor(t, half):
-            nc.vector.tensor_tensor(
-                floored[half][:, t, :], banks[COMMAND_BANKS[half][t]][:], bounds[LOWER][half][:, t, :], ALU.max
-            )
+            for j0, j1 in ((0, HALF // 2), (HALF // 2, HALF)) if t == TILES - 1 else ((0, HALF),):
+                nc.vector.tensor_tensor(
+                    floored[half][:, t, j0:j1],
+                    banks[COMMAND_BANKS[half][t]][:, j0:j1],
+                    bounds[LOWER][half][:, t, j0:j1],
+                    ALU.max,
+                )
 
         def command(t, half):
             command_pass(t, half, 1, True)
             command_pass(t, half, 0, False)
 
         def clamp(g):
-            j0, j1 = GROUPS[g]
-            half = j0 // HALF
-            columns = slice(j0 - HALF * half, j1 - HALF * half)
-            nc.vector.tensor_tensor(
-                h_bf[g][:].rearrange("p (m x t) -> p m t x", x=4, t=TILES),
-                floored[half][:, :, columns].rearrange("p t (m x) -> p m t x", x=4),
-                bounds[UPPER][half][:, :, columns].rearrange("p t (m x) -> p m t x", x=4),
-                ALU.min,
-            )
+            g0, g1 = GROUPS[g]
+            half = g0 // HALF
+            for j0 in range(g0, g1, HALF // 2):
+                j1 = min(g1, j0 + HALF // 2)
+                columns = slice(j0 - HALF * half, j1 - HALF * half)
+                nc.vector.tensor_tensor(
+                    h_bf[g][:, TILES * (j0 - g0) : TILES * (j1 - g0)].rearrange("p (m x t) -> p m t x", x=4, t=TILES),
+                    floored[half][:, :, columns].rearrange("p t (m x) -> p m t x", x=4),
+                    bounds[UPPER][half][:, :, columns].rearrange("p t (m x) -> p m t x", x=4),
+                    ALU.min,
+                )
 
         def quantise_h(g):
             nc.vector.quantize_mx(out=h_w[g][:].bitcast(E4M3X4), scales=h_s[g][:], in_=h_bf[g][:])
@@ -290,11 +296,11 @@ def tile_list_clamped_scenario_commands_kernel(
         quantise_wc(0, 2, 4)
         for t in range(2):
             command_pass(t, 0, 0, True)
-        bound(LOWER, 2, 1)
         round_wc(1, 0, 4)
         round_wc(2, 0, 2)
         round_wc(2, 2, 4)
-        quantise_wc(1, 0, 2)
+        quantise_wc(1, 0, 1)
+        quantise_wc(1, 1, 2)
         quantise_wc(1, 2, 4)
 
         for t in range(2):
@@ -303,7 +309,8 @@ def tile_list_clamped_scenario_commands_kernel(
         for t in range(2, TILES):
             command(t, 0)
             floor(t, 0)
-        bound(LOWER, 3, 1)
+        for t in range(2, TILES):
+            bound(LOWER, t, 1)
         nc.scalar.copy(
             out=wy_bf[:].rearrange("p (m x t) -> p m t x", x=4, t=TILES),
             in_=wy_raw[:].rearrange("p t (m x) -> p m t x", x=4),

@@ -44,9 +44,10 @@ AT_WC1B = AT_WHI + WORDS - OVERLAP
 WC_PIECES = ((0, 0, H), (1, 0, H // 2), (1, H // 2, H))
 AT_WC = (AT_WC0, AT_WC1A, AT_WC1B)
 
-BOUND_BANKS = (((0, 1, 2, 3), (0, 1, 2, 3)), ((4, 5, 6, 7), (0, 1, 4, 5)))
-COMMAND_BANKS = ((2, 3, 4, 5), (6, 7, 2, 3))
-OUTPUT_BANKS = (6, 0, 1, 4, 7, 5, 2, 3)
+BOUND_BANKS = (((0, 1, 2, 3), (0, 1, 2, 3)), ((4, 5, 6, 7), (0, 1, 2, 3)))
+COMMAND_BANKS = ((2, 3, 4, 5), (6, 7, 4, 5))
+OUTPUT_BANKS = (6, 0, 1, 7, 4, 2, 5, 3)
+EARLY_TILES = 2
 
 GROUPS = ((0, HALF),) + tuple((j0, j0 + P) for j0 in range(HALF, S, P))
 VECTOR_BLOCKS = ((3, 1), (3, 2), (4, 1))
@@ -152,10 +153,13 @@ def tile_list_clamped_scenario_commands_kernel(
             for w in range(2)
         ]
 
-        def bound_out(w, t, half):
+        def bound_out(w, t, half, j0=0, j1=HALF):
             column = QUAD * t + w
             nc.scalar.activation(
-                bounds[w][half][:, t, :], banks[BOUND_BANKS[w][half][t]][:], ACT.Identity, bias=bias[:, column : column + 1]
+                bounds[w][half][:, t, j0:j1],
+                banks[BOUND_BANKS[w][half][t]][:, j0:j1],
+                ACT.Identity,
+                bias=bias[:, column : column + 1],
             )
 
         def bound(w, t, half):
@@ -190,7 +194,7 @@ def tile_list_clamped_scenario_commands_kernel(
             for t in range(TILES):
                 bound_out(w, t, 0)
         gather_words(1, 1)
-        for t in range(2):
+        for t in range(EARLY_TILES):
             bound(LOWER, t, 1)
 
         wy_raw = shared.tile([P, TILES, N], F32, name="wy_raw", offset=AT_SECOND_PASS, align_bytes=64)
@@ -294,7 +298,7 @@ def tile_list_clamped_scenario_commands_kernel(
         round_wc(0, 2, 4)
         quantise_wc(0, 0, 2)
         quantise_wc(0, 2, 4)
-        for t in range(2):
+        for t in range(EARLY_TILES):
             command_pass(t, 0, 0, True)
         round_wc(1, 0, 4)
         round_wc(2, 0, 2)
@@ -303,23 +307,27 @@ def tile_list_clamped_scenario_commands_kernel(
         quantise_wc(1, 1, 2)
         quantise_wc(1, 2, 4)
 
-        for t in range(2):
+        for t in range(EARLY_TILES):
             command_pass(t, 0, 1, False)
             floor(t, 0)
-        for t in range(2, TILES):
+        for t in range(EARLY_TILES, TILES):
             command(t, 0)
             floor(t, 0)
-        for t in range(2, TILES):
+        for t in range(EARLY_TILES, TILES):
             bound(LOWER, t, 1)
         nc.scalar.copy(
             out=wy_bf[:].rearrange("p (m x t) -> p m t x", x=4, t=TILES),
             in_=wy_raw[:].rearrange("p t (m x) -> p m t x", x=4),
         )
-        bound(UPPER, 0, 1)
+
+        command(0, 1)
         for t in range(1, TILES):
-            bound(UPPER, t, 1)
-            command(t - 1, 1)
-        command(3, 1)
+            command(t, 1)
+            bound(UPPER, t - 1, 1)
+        for a in range(PASSES):
+            bound_pass(UPPER, TILES - 1, 1, a)
+        bound_out(UPPER, TILES - 1, 1, 0, P)
+        bound_out(UPPER, TILES - 1, 1, P, HALF)
         clamp(0)
         floor(0, 1)
         quantise_h(0)

@@ -46,7 +46,7 @@ AT_WC = (AT_WC0, AT_WC1A, AT_WC1B)
 
 BOUND_BANKS = (((0, 1, 2, 3), (0, 1, 2, 3)), ((4, 5, 6, 7), (0, 1, 2, 3)))
 COMMAND_BANKS = ((2, 3, 4, 5), (6, 7, 4, 5))
-OUTPUT_BANKS = (6, 0, 1, 7, 4, 2, 5, 3)
+OUTPUT_BANKS = ((6, 7, 5), (4, 6, 7), (0, 1, 2), (3, 5, 4), (6, 7, 0))
 EARLY_TILES = 2
 
 GROUPS = ((0, HALF),) + tuple((j0, j0 + P) for j0 in range(HALF, S, P))
@@ -273,7 +273,7 @@ def tile_list_clamped_scenario_commands_kernel(
 
         def outputs(g):
             j0, j1 = GROUPS[g]
-            sums = [banks[OUTPUT_BANKS[(BLOCKS * g + c) % 8]][:, 0 : j1 - j0] for c in range(BLOCKS)]
+            sums = [banks[b][:, 0 : j1 - j0] for b in OUTPUT_BANKS[g]]
             for c in range(BLOCKS):
                 nc.tensor.matmul_mx(
                     out=sums[c],

from contextlib import ExitStack

import concourse.mybir as mybir

K, H, N, T, S = 1024, 512, 384, 4096, 1024
FLOPS = 2 * 3 * K * H * S + 2 * H * N * S

F32 = mybir.dt.float32
BF16 = mybir.dt.bfloat16
I32 = mybir.dt.int32
U32 = mybir.dt.uint32
U16 = mybir.dt.uint16
U8 = mybir.dt.uint8
E4M3X4 = mybir.dt.float8_e4m3fn_x4
E2M1X4 = mybir.dt.float4_e2m1fn_x4
ALU = mybir.AluOpType
ACT = mybir.ActivationFunctionType

P = 128
PASSES = K // 512
HALF = 512
TILES = 4
BLOCKS = N // P
LOWER, UPPER = 0, 1
SCALE_ROWS = 16 * PASSES
QUAD = 32

STATE_SCALES = S // 4
WEIGHT_SCALES = H // 4
PLANE_WIDTH = STATE_SCALES + 2 * WEIGHT_SCALES

OVERLAP = 64
WORDS = PASSES * 2 * H
AT_DEALT_WORDS = 0
AT_PICKED_SCALES = AT_DEALT_WORDS + 2 * WORDS - OVERLAP
AT_SECOND_PASS = AT_PICKED_SCALES + S - OVERLAP
AT_SCALE_ROWS = AT_SECOND_PASS + 4 * T
AT_WC0 = AT_SCALE_ROWS + T
AT_WLO = AT_WC0 + 16 * H - OVERLAP
AT_WC1A = AT_WLO + WORDS - OVERLAP
AT_WHI = AT_WC1A + 8 * H
AT_WC1B = AT_WHI + WORDS - OVERLAP

WC_PIECES = ((0, 0, H), (1, 0, H // 2), (1, H // 2, H))
AT_WC = (AT_WC0, AT_WC1A, AT_WC1B)

BOUND_BANKS = (((0, 1, 2, 3), (0, 1, 2, 3)), ((4, 5, 6, 7), (0, 1, 2, 3)))
COMMAND_BANKS = ((2, 3, 4, 5), (6, 7, 4, 5))
OUTPUT_BANKS = ((6, 7, 5), (4, 6, 7), (0, 1, 2), (3, 5, 4), (6, 7, 0))
EARLY_TILES = 2

GROUPS = ((0, HALF),) + tuple((j0, j0 + P) for j0 in range(HALF, S, P))
VECTOR_BLOCKS = ((3, 1), (3, 2), (4, 1))


def tile_list_clamped_scenario_commands_kernel(
    tc, tab_words, tab_scales, offs, wc, wlo_words, wlo_scales, whi_words, whi_scales, blo, bhi, wy, by, out
):
    nc = tc.nc
    with ExitStack() as ctx:
        keep = ctx.enter_context(tc.tile_pool(name="keep", bufs=1))
        psum = ctx.enter_context(tc.psum_pool(name="psum", bufs=1))
        banks = [psum.tile([P, HALF], F32, name=f"bank{b}") for b in range(8)]
        shared = ctx.enter_context(tc.tile_pool(name="shared", bufs=1))

        offsets = keep.tile([P, S // 16], U16, name="offsets")
        nc.sync.dma_start(offsets[:], offs)
        tab_s = shared.tile([P, T // 4], I32, name="tab_s", offset=AT_SCALE_ROWS, align_bytes=64)
        nc.sync.dma_start(tab_s[0:SCALE_ROWS], tab_scales.rearrange("a q e -> (a q) e").bitcast(I32))
        bound_s_raw = keep.tile([P, 2, WEIGHT_SCALES], I32, name="bound_s_raw", align_bytes=64)
        for w, scales in enumerate((wlo_scales, whi_scales)):
            nc.sync.dma_start(bound_s_raw[0:SCALE_ROWS, w], scales.rearrange("a q e -> (a q) e").bitcast(I32))
        bound_w_raw = [
            shared.tile([P, PASSES, H // 2], I32, name=f"bound_w_raw{w}", offset=at, align_bytes=64)
            for w, at in enumerate((AT_WLO, AT_WHI))
        ]
        for w, words in enumerate((wlo_words, whi_words)):
            nc.sync.dma_start(bound_w_raw[w][:], words.rearrange("a p e -> p a e").bitcast(I32))
        tab_w = [keep.tile([P, T], I32, name="tab_w0", align_bytes=64)]
        nc.sync.dma_start(tab_w[0][:], tab_words[0].rearrange("p e j -> p (e j)").bitcast(I32))

        bias_raw = keep.tile([P, P], F32, name="bias_raw", align_bytes=64)
        bias_rows = keep.tile([P, 2 * P], F32, name="bias_rows", align_bytes=64)
        nc.gpsimd.memset(bias_raw[:], 0.0)
        nc.gpsimd.memset(bias_rows[:, P : 2 * P], 0.0)
        for w, vector in enumerate((blo, bhi)):
            nc.sync.dma_start(bias_raw[w:P:QUAD, :], vector.rearrange("(q x) -> q x", q=4))
        nc.sync.dma_start(
            bias_rows[0:P:QUAD, P : P + QUAD * BLOCKS].rearrange("q (c x) -> q c x", c=BLOCKS),
            by.rearrange("(c q x) -> q c x", c=BLOCKS, q=4),
        )

        planes = [keep.tile([P, PLANE_WIDTH], I32, name="planes0", align_bytes=64)]
        for p0, p1 in ((SCALE_ROWS, 64), (64, P)):
            nc.vector.memset(tab_s[p0:p1], 0)
        for p0, p1 in ((SCALE_ROWS, 64), (64, P)):
            nc.gpsimd.memset(bound_s_raw[p0:p1], 0)

        picked_s = shared.tile([P, S], U8, name="picked_s", offset=AT_PICKED_SCALES, align_bytes=64)
        nc.vector.tensor_copy(picked_s[:], tab_s[:].bitcast(U8).indirect(offsets[:]))
        nc.vector.tensor_copy(
            out=planes[0][:, STATE_SCALES:PLANE_WIDTH].rearrange("p (w t u) -> p w t u", w=2, t=TILES),
            in_=bound_s_raw[:].rearrange("p w (u t) -> p w t u", t=TILES),
        )
        nc.vector.tensor_copy(out=planes[0][:, 0:STATE_SCALES], in_=picked_s[:].bitcast(I32))
        for quadrant in range(1, 4):
            nc.sync.dma_start(
                planes[0][32 * quadrant : 32 * quadrant + 4], planes[0][4 * quadrant : 4 * quadrant + 4]
            )
        tab_w.append(shared.tile([P, T], I32, name="tab_w1", offset=AT_SECOND_PASS, align_bytes=64))
        nc.sync.dma_start(tab_w[1][:], tab_words[1].rearrange("p e j -> p (e j)").bitcast(I32))
        planes.append(shared.tile([P, PLANE_WIDTH], I32, name="planes1", offset=AT_SCALE_ROWS, align_bytes=64))
        nc.vector.memset(planes[1][:], 0)
        for quadrant in range(4):
            nc.sync.dma_start(
                planes[1][32 * quadrant : 32 * quadrant + 4], planes[0][16 + 4 * quadrant : 20 + 4 * quadrant]
            )

        bound_w = shared.tile([P, 2, PASSES, H // 2], I32, name="bound_w", offset=AT_DEALT_WORDS, align_bytes=64)
        for w in range(2):
            nc.vector.tensor_copy(
                out=bound_w[:, w].rearrange("p a (t u x) -> p a t u x", t=TILES, x=2),
                in_=bound_w_raw[w][:].rearrange("p a (u t x) -> p a t u x", t=TILES, x=2),
            )

        bias = keep.tile([P, 2 * P], F32, name="bias", align_bytes=64)
        v_w = [
            [keep.tile([P, HALF], U32, name=f"v_w{a}{half}", align_bytes=64) for half in range(2)]
            for a in range(PASSES)
        ]

        def gather_words(a, half):
            columns = slice(HALF // 16 * half, HALF // 16 * (half + 1))
            nc.vector.tensor_copy(v_w[a][half][:], tab_w[a][:].bitcast(U32).indirect(offsets[:, columns]))

        def state_scales(a, half):
            return planes[a][:, HALF // 4 * half : HALF // 4 * (half + 1)].bitcast(U8)

        def bound_pass(w, t, half, a):
            scales_at = STATE_SCALES + WEIGHT_SCALES * w + P // 4 * t
            nc.tensor.matmul_mx(
                out=banks[BOUND_BANKS[w][half][t]][:],
                lhsT=bound_w[:, w, a, P // 2 * t : P // 2 * (t + 1)].bitcast(U8).bitcast(E2M1X4),
                lhsT_scale=planes[a][:, scales_at : scales_at + P // 4].bitcast(U8),
                rhs=v_w[a][half][:].bitcast(E4M3X4),
                rhs_scale=state_scales(a, half),
                start=(a == 0),
                stop=(a == PASSES - 1),
            )

        bounds = [
            [keep.tile([P, TILES, HALF], F32, name=f"bounds{w}{half}", align_bytes=64) for half in range(2)]
            for w in range(2)
        ]

        def bound_out(w, t, half, j0=0, j1=HALF):
            column = QUAD * t + w
            nc.scalar.activation(
                bounds[w][half][:, t, j0:j1],
                banks[BOUND_BANKS[w][half][t]][:, j0:j1],
                ACT.Identity,
                bias=bias[:, column : column + 1],
            )

        def bound(w, t, half):
            for a in range(PASSES):
                bound_pass(w, t, half, a)
            bound_out(w, t, half)

        gather_words(0, 1)
        gather_words(0, 0)
        for w in (LOWER, UPPER):
            for t in range(TILES):
                bound_pass(w, t, 0, 0)

        nc.vector.tensor_copy(
            out=bias_rows[:, 0:P].rearrange("p (t u i) -> p t u i", t=TILES, i=4),
            in_=bias_raw[:].rearrange("p (u t i) -> p t u i", t=TILES, i=4),
        )
        nc.vector.transpose(bias[:], bias_rows[:])

        wc_rows = wc.rearrange("(a p j) r -> a p j r", p=P, j=4)
        wc_raw = []
        for (a, r0, r1), at in zip(WC_PIECES, AT_WC):
            piece = shared.tile([P, 4, r1 - r0], F32, name=f"wc_raw{a}_{r0}", offset=at, align_bytes=64)
            nc.sync.dma_start(piece[:], wc_rows[a, :, :, r0:r1])
            wc_raw.append(piece)

        gather_words(1, 0)
        for w in (LOWER, UPPER):
            for t in range(TILES):
                bound_pass(w, t, 0, 1)
        for w in (LOWER, UPPER):
            for t in range(TILES):
                bound_out(w, t, 0)
        gather_words(1, 1)
        for t in range(EARLY_TILES):
            bound(LOWER, t, 1)

        wy_raw = shared.tile([P, TILES, N], F32, name="wy_raw", offset=AT_SECOND_PASS, align_bytes=64)
        wy_rows = wy.rearrange("(u t i) n -> t u i n", t=TILES, i=4)
        for t in range(TILES):
            nc.sync.dma_start(wy_raw[:, t, :], wy_rows[t])

        wc_bf = [keep.tile([P, H * 4], BF16, name=f"wc_bf{a}", align_bytes=64) for a in range(PASSES)]
        wc_w = [keep.tile([P, H], U32, name=f"wc_w{a}", align_bytes=64) for a in range(PASSES)]
        wc_s = [keep.tile([P, H], U8, name=f"wc_s{a}", align_bytes=64) for a in range(PASSES)]

        def round_wc(piece, t0, t1):
            a, r0, r1 = WC_PIECES[piece]
            dealt = wc_bf[a][:].rearrange("p (t u i j) -> p t u j i", t=TILES, i=4, j=4)
            nc.vector.tensor_copy(
                out=dealt[:, t0:t1, r0 // 16 : r1 // 16],
                in_=wc_raw[piece][:].rearrange("p j (u t i) -> p t u j i", t=TILES, i=4)[:, t0:t1],
            )

        def quantise_wc(a, t0, t1):
            nc.vector.quantize_mx(
                out=wc_w[a][:, P * t0 : P * t1].bitcast(E4M3X4),
                scales=wc_s[a][:, P * t0 : P * t1],
                in_=wc_bf[a][:, 4 * P * t0 : 4 * P * t1],
            )

        wy_bf = keep.tile([P, N * TILES], BF16, name="wy_bf", align_bytes=64)
        wy_s = keep.tile([P, N], U8, name="wy_s", align_bytes=64)

        floored = [keep.tile([P, TILES, HALF], F32, name=f"floored{half}") for half in range(2)]
        h_bf = [keep.tile([P, (j1 - j0) * TILES], BF16, name=f"h_bf{j0}", align_bytes=64) for j0, j1 in GROUPS]
        h_w = [keep.tile([P, j1 - j0], U32, name=f"h_w{j0}", align_bytes=64) for j0, j1 in GROUPS]
        h_s = [keep.tile([P, j1 - j0], U8, name=f"h_s{j0}", align_bytes=64) for j0, j1 in GROUPS]
        y = [keep.tile([P, BLOCKS, j1 - j0], F32, name=f"y{j0}") for j0, j1 in GROUPS]
        out_rows = out.rearrange("(c p) s -> p c s", p=P)

        def command_pass(t, half, a, opens):
            nc.tensor.matmul_mx(
                out=banks[COMMAND_BANKS[half][t]][:],
                lhsT=wc_w[a][:, P * t : P * (t + 1)].bitcast(E4M3X4),
                lhsT_scale=wc_s[a][:, P * t : P * (t + 1)],
                rhs=v_w[a][half][:].bitcast(E4M3X4),
                rhs_scale=state_scales(a, half),
                start=opens,
                stop=not opens,
            )

        def floor(t, half):
            for j0, j1 in ((0, HALF // 2), (HALF // 2, HALF)) if t == TILES - 1 else ((0, HALF),):
                nc.vector.tensor_tensor(
                    floored[half][:, t, j0:j1],
                    banks[COMMAND_BANKS[half][t]][:, j0:j1],
                    bounds[LOWER][half][:, t, j0:j1],
                    ALU.max,
                )

        def command(t, half):
            command_pass(t, half, 1, True)
            command_pass(t, half, 0, False)

        def clamp(g):
            g0, g1 = GROUPS[g]
            half = g0 // HALF
            for j0 in range(g0, g1, HALF // 2):
                j1 = min(g1, j0 + HALF // 2)
                columns = slice(j0 - HALF * half, j1 - HALF * half)
                nc.vector.tensor_tensor(
                    h_bf[g][:, TILES * (j0 - g0) : TILES * (j1 - g0)].rearrange("p (m x t) -> p m t x", x=4, t=TILES),
                    floored[half][:, :, columns].rearrange("p t (m x) -> p m t x", x=4),
                    bounds[UPPER][half][:, :, columns].rearrange("p t (m x) -> p m t x", x=4),
                    ALU.min,
                )

        def quantise_h(g):
            nc.vector.quantize_mx(out=h_w[g][:].bitcast(E4M3X4), scales=h_s[g][:], in_=h_bf[g][:])

        def outputs(g):
            j0, j1 = GROUPS[g]
            sums = [banks[b][:, 0 : j1 - j0] for b in OUTPUT_BANKS[g]]
            for c in range(BLOCKS):
                nc.tensor.matmul_mx(
                    out=sums[c],
                    lhsT=wy_w[:, P * c : P * (c + 1)].bitcast(E4M3X4),
                    lhsT_scale=wy_s[:, P * c : P * (c + 1)],
                    rhs=h_w[g][:].bitcast(E4M3X4),
                    rhs_scale=h_s[g][:],
                    start=True,
                    stop=True,
                )
            for c in range(BLOCKS):
                if (g, c) in VECTOR_BLOCKS:
                    nc.vector.tensor_scalar(y[g][:, c, :], sums[c], bias[:, P + QUAD * c : P + QUAD * c + 1], None, ALU.add)
                else:
                    nc.scalar.activation(y[g][:, c, :], sums[c], ACT.Identity, bias=bias[:, P + QUAD * c : P + QUAD * c + 1])
                if g == 0:
                    nc.sync.dma_start(out_rows[:, c, j0:j1], y[g][:, c, :])
            if g > 0:
                nc.sync.dma_start(out_rows[:, :, j0:j1], y[g][:])

        round_wc(0, 0, 2)
        round_wc(0, 2, 4)
        quantise_wc(0, 0, 2)
        quantise_wc(0, 2, 4)
        for t in range(EARLY_TILES):
            command_pass(t, 0, 0, True)
        round_wc(1, 0, 4)
        round_wc(2, 0, 2)
        round_wc(2, 2, 4)
        quantise_wc(1, 0, 1)
        quantise_wc(1, 1, 2)
        quantise_wc(1, 2, 4)

        for t in range(EARLY_TILES):
            command_pass(t, 0, 1, False)
            floor(t, 0)
        for t in range(EARLY_TILES, TILES):
            command(t, 0)
            floor(t, 0)
        for t in range(EARLY_TILES, TILES):
            bound(LOWER, t, 1)
        nc.scalar.copy(
            out=wy_bf[:].rearrange("p (m x t) -> p m t x", x=4, t=TILES),
            in_=wy_raw[:].rearrange("p t (m x) -> p m t x", x=4),
        )

        command(0, 1)
        for t in range(1, TILES):
            command(t, 1)
            bound(UPPER, t - 1, 1)
        for a in range(PASSES):
            bound_pass(UPPER, TILES - 1, 1, a)
        bound_out(UPPER, TILES - 1, 1, 0, P)
        bound_out(UPPER, TILES - 1, 1, P, HALF)
        clamp(0)
        floor(0, 1)
        quantise_h(0)

        wy_w = keep.tile([P, N], U32, name="wy_w", tag="bounds00", align_bytes=64)
        for n0, n1 in ((0, 256), (256, N)):
            nc.vector.quantize_mx(
                out=wy_w[:, n0:n1].bitcast(E4M3X4), scales=wy_s[:, n0:n1], in_=wy_bf[:, TILES * n0 : TILES * n1]
            )

        for t in range(1, TILES):
            floor(t, 1)
        outputs(0)
        clamp(1)
        for g in (1, 2):
            clamp(g + 1)
            quantise_h(g)
            outputs(g)
        clamp(4)
        quantise_h(3)
        quantise_h(4)
        outputs(3)
        outputs(4)
